import numpy as np, ml_dtypes
CORES = [8,136,40,168]
N = 4
BF = ml_dtypes.bfloat16
def gentries(a):
    return np.ascontiguousarray(a.reshape(8, 16, -1).transpose(0, 2, 1)).reshape(8, -1)
def gtable(e):
    e = np.asarray(e); return np.ascontiguousarray(e.reshape(8, -1, 16).transpose(0, 2, 1)).reshape(128, -1).astype(np.int32)
G, C, P, RO, YC = 64, 64, 128, 3, 32
W, LG, LC, H, M = 4096, 6, 6, 32, 16
BIG = 2 ** 24
def probes(u, k):
    return (((u * u) >> 5)[..., None] + u[..., None] * k) & (W - 1)
def base(rng):
    ring = rng.integers(0, 256, (8, 8, 64, 16)); a = rng.integers(0, 8, (N, 8, G, 1)); b = rng.integers(0, 64, (N, 8, G, 1))
    X = ring[np.arange(8)[None, :, None, None], a, (b + np.arange(C)) & 63]
    X = np.clip(X + rng.integers(-4, 5, X.shape), 0, 255)
    th = np.where(rng.random((N, 8, P)) < 0.25, rng.integers(0, 300, (N, 8, P)), rng.integers(600, 1600, (N, 8, P)))
    return X, rng.integers(1, 256, (N, 8, 16)), rng.integers(0, 2048, (N, 8, RO, P)), th
def pack(X, wt, km, th):
    X = np.ascontiguousarray(X.reshape(N, 8, G, C, 16).transpose(0, 1, 4, 2, 3)).reshape(N, 128, W)
    return {"gen0": X.astype(np.float32).astype(BF), "wt": np.ascontiguousarray(wt.reshape(N, 128, 1)).astype(np.int32),
            "km": np.stack([gtable(a.reshape(8, -1)) for a in km]), "th": np.stack([gtable(a) for a in th])}
def setup_inputs(rng):
    return pack(*base(rng))
def column(rng, w, u):
    x = rng.integers(0, 256, 16); r = (int(u) - int(np.sum(w[2:] * x[2:]))) & (W - 1); x[0] = r & 15; x[1] = r >> 4
    return x
def link(rng, Y, w, k, o, alone=False):
    c = probes(np.arange(W)[None, :], k[None, None, :])[0]
    od = np.argsort(c.reshape(-1).astype(np.int16), kind="stable"); st = np.searchsorted(c.reshape(-1)[od], np.arange(W + 1))
    for i in range(G - 1):
        if alone and i == 1: continue
        j = 2 if alone and i == 0 else i + 1
        t = C * j + int(o[i]); us = od[st[t]:st[t + 1]] // P; us = us[~np.any(c[us] == C * i + C - 1, axis=1)]
        if len(us):
            x = column(rng, w, us[int(rng.integers(0, len(us)))]); Y[i, C - 1] = x; Y[j, int(o[i])] = x
def setup_inputs_deep(rng):
    X, wt, km, th = base(rng); th = rng.integers(30, 41, th.shape); B = 8 * N; b = np.arange(B)
    X = X.reshape(B, G, C, 16); w = wt.reshape(B, 1, 16).astype(np.int32); k0 = km[:, :, 0].reshape(B, 1, P).astype(np.int32); tries = min(128, max(16, 16 * G // P))
    for i in range(G - 1):
        x = rng.integers(0, 256, (B, tries, 16), dtype=np.int32); u = (np.sum(w * x, axis=2) & (W - 1)).astype(np.int32)
        c = probes(u, k0); o = c & (C - 1); to = np.where((b % 4 == 2) & (i == 0), 2, i + 1)
        hit = ((c >> LC) == to[:, None, None]) & (o != C - 1) & ~np.any(c == C * i + C - 1, axis=2)[..., None]
        like = np.where((b % 4 == 0)[:, None, None], o, np.where((b % 4 == 2)[:, None, None], C - 1 - o, 0)) + 1
        s = np.where(hit, like, 0).reshape(B, -1); a = np.argmax(s, axis=1)
        do = (s[b, a] > 0) & ((b % 2 == 0) | (rng.random(B) < 0.9)) & ((b % 4 != 2) | (i != 1))
        bb = b[do]; aa = a[do]; xs = x[bb, aa // P]
        X[bb, i, C - 1] = xs; X[bb, to[bb], o.reshape(B, -1)[bb, aa]] = xs
    X = X.reshape(N, 8, G, C, 16)
    for g in (3, 4, 7):
        wt[:, g, 0] = 1; wt[:, g, 1] = 16
    for r in range(N): link(rng, X[r, 4], wt[r, 4], km[r, 4, 0], np.full(G, C - 2))
    k = np.arange(2048)
    for g in (3, 7):
        h = int(rng.choice(np.array([3, 5, 7, 9]))); q0 = int(np.argmin((np.arange(C) * h + 1) & (C - 1))); Y = X[:, g].copy()
        for r in range(N):
            u = h - 1 + H * int(rng.integers(0, W // H)); c = (u * u // 32 + k * u) & (W - 1)
            km[r, g, 0] = rng.choice(k[(c & (C - 1)) != C - 1], P); Y[:, r * M:(r + 1) * M, q0] = column(rng, wt[r, g], u)
        for d in range(N): link(rng, Y[d], wt[d, g], km[d, g, 1], np.full(G, C - 2) if g == 3 else 2 * rng.integers(0, C // 2, G), g == 7)
        p = (C * np.arange(G)[:, None] + h * np.arange(C)) & (W - 1)
        for r in range(N):
            kid = np.zeros((G, C, 16), np.int64)
            for d in range(N): kid[(d - r) % N::N] = Y[d, r * M:(r + 1) * M]
            X[r, g, p >> LC, p & (C - 1)] = kid
    return pack(X, wt, km, th)
def setup_inputs_edges(rng):
    X, wt, km, th = base(rng)
    th[:, 0] = 0; e = X[:, 0, :1, C - 1].copy(); X[:, 0, ::2, C - 1] = e; X[:, 0, :, ::4] = e[:, :, None]
    f = rng.integers(0, 16, (N, G, C, 1)); X[:, 1] = (np.arange(16) == f) & (rng.random((N, G, C, 1)) < 0.2); X[:, 1, :, C - 1] = 255; th[:, 1] = 4080
    k = np.arange(2048)
    for q in range(N):
        u = int(255 * np.sum(wt[q, 1])) & (W - 1); c = ((u * u >> 5) + k * u) & (W - 1)
        good = k[(c & (C - 1)) != C - 1]
        km[q, 1, 0] = rng.choice(good if len(good) else k, P)
    km[:, 2] = rng.choice(np.array([0, 1, 3, 2047]), (N, RO, P))
    X[:, 3, ::2, C - 1] = 0; X[:, 3, 0, 0] = 0
    wt[:, 4] = 255; X[:, 4] = 255 - rng.integers(0, 3, (N, G, C, 16))
    X[:, 5, :, C - 1] = rng.integers(0, 256, (N, 1, 16))
    X[:, 6] = 255 * rng.integers(0, 2, (N, G, C, 16)); th[:, 6] = 255 * rng.integers(2, 9, (N, P))
    return pack(X, wt, km, th)
def setup_inputs_far(rng):
    X, wt, km, th = base(rng); k = np.arange(2048)
    for q in range(N):
        for g in (0, 1, 2, 4, 5):
            wt[q, g, 0] |= 1; wt[q, g, 8:] = wt[q, g, :8]
            b = np.concatenate([rng.integers(110, 181, (256, 8)), rng.integers(80, 101, (256, 8))], axis=1); u = np.sum(wt[q, g] * b, axis=1) & (W - 1)
            c = probes(u[None, :], k[None, None, :])[0]
            ok = (c == W - 1) if g == 4 else (c >= 3 * W // 4) & ((c & (C - 1)) != C - 1)
            if g == 5: ok = ok & np.any(c == 0, axis=1)[:, None]
            a, m = np.nonzero(ok); s = int(rng.integers(0, len(a))); x = b[a[s]]; c = c[a[s]]; K = int(m[s]); j = int(c[K]) >> LC; o = int(c[K]) & (C - 1)
            e = rng.integers(35, 71, (G, 8)); e[G // 4:G // 2] = rng.integers(0, 35, (G // 2 - G // 4, 8))
            if g > 2: e[:] = 0
            last = x + np.concatenate([e, -e], axis=1); X[q, g, :, C - 1] = last; km[q, g, 0] = K
            if g == 1:
                km[q, 1, 0] = rng.choice(k[(c & (C - 1)) != C - 1], P); th[q, 1] = rng.integers(2048, 4081, P)
                X[q, 1, :, :C - 1, :8] = rng.integers(0, 41, (G, C - 1, 8)); X[q, 1, :, :C - 1, 8:] = rng.integers(215, 256, (G, C - 1, 8))
            elif g == 4:
                d = rng.integers(1, 60, 16); X[q, 4, G - 1, C - 1] = x - d; th[q, 4] = int(np.sum(d)) + 1
            elif g == 5:
                d = rng.integers(1, 30, 16); X[q, 5, 0, 0] = x - d; X[q, 5, j, o] = x - rng.integers(30, 60, 16)
                km[q, 5, 0, ::2] = int(np.argmax(c == 0)); th[q, 5] = 4080; th[q, 5, ::2] = int(np.sum(d))
            else:
                v = np.repeat(np.array([0, 255]), 8); X[q, g, j, o] = v
                th[q, g] = 4080 if g == 0 else int(np.min(np.sum(np.abs(last - v), axis=1)))
    X[:, 3] = 255 - rng.integers(0, 64, (N, G, C, 16)); X[:, 3, :, C - 1] = rng.integers(0, 64, (N, G, 16)); th[:, 3] = rng.integers(2048, 4081, (N, P))
    return pack(X, wt, km, th)
def setup_inputs_spread(rng):
    X, wt, km, th = base(rng)
    X = np.minimum((rng.random((N, 8, G, C, 16)) * np.exp2(rng.integers(0, 9, (N, 8, G, C, 1)))).astype(np.int64), 255)
    wt = np.clip(np.exp2(8 * rng.random(wt.shape)).astype(np.int64), 1, 255); km = np.clip(np.exp2(11 * rng.random(km.shape)).astype(np.int64) - 1, 0, 2047); km[..., ::2] = rng.integers(0, 2048, km[..., ::2].shape)
    th = rng.integers(0, 4081, th.shape)
    return pack(X, wt, km, th)
def setup_inputs_ties(rng):
    X, wt, km, th = base(rng)
    pat = rng.integers(1, 254, (8, 4, 16)); a = rng.integers(0, 4, (N, 8, G, C))
    X = pat[np.arange(8)[None, :, None, None], a] + rng.integers(0, 2, (N, 8, G, C, 16)); th = rng.integers(3, 11, th.shape)
    return pack(X, wt, km, th)
def check_inputs(d):
    bad = []; v = np.asarray(d["gen0"]).astype(np.float32)
    if not np.all((v >= 0) & (v <= 255) & (v == np.floor(v))): bad.append("gen0 holds other numbers than 0 .. 255")
    for k, lo, hi in (("wt", 1, 255), ("km", 0, 2047), ("th", 0, 4080)):
        if np.min(d[k]) < lo or np.max(d[k]) > hi: bad.append("range of " + k)
    return bad
def reference(gen0, wt, km, th):
    B = 8 * N; X = gen0.astype(np.float32).astype(np.int32).reshape(B, 16, W); w = wt.astype(np.int64).reshape(B, 16, 1)
    kl = np.stack([gentries(a) for a in km]).astype(np.int64).reshape(B, RO, P); tl = np.stack([gentries(a) for a in th]).astype(np.int64).reshape(B, 1, P)
    ar = np.arange(G); q = np.arange(C); rows = np.arange(B)[:, None]
    for t in range(RO):
        x = X[:, :, C - 1::C]
        u = np.sum(w * x, axis=1) & (W - 1)
        c = probes(u, kl[:, t][:, None, :])
        pr = np.take_along_axis(X, c.reshape(B, 1, G * P), 2).reshape(B, 16, G, P)
        D = np.sum(np.abs(pr - x[..., None]), axis=1).astype(np.int64)
        best = np.min(np.where(D < tl, D * W + c, BIG), axis=2)
        j = (best & (W - 1)) >> LC; o = best & (C - 1); ok = (best < BIG) & (j > ar)
        acc = np.full((B, G), BIG, np.int64)
        np.minimum.at(acc, (rows, np.where(ok, j, 0)), np.where(ok, (best - (best & (W - 1))) + ar * C + o, BIG))
        got = acc < BIG; cut = np.where(got, 1 + ((acc & (C - 1)) >> 1), 0); ln = C - cut
        root = np.where(got, (acc & (W - 1)) >> LC, ar)
        for _ in range(LG): root = np.take_along_axis(root, root, 1)
        od = np.argsort(root * G + ar, axis=1)
        ls = np.take_along_axis(ln, od, 1); pos = np.zeros((B, G), np.int64)
        np.put_along_axis(pos, od, np.add.accumulate(ls, axis=1) - ls, 1); L = np.sum(ln, axis=1)
        place = np.where(q < cut[..., None], W, pos[..., None] + q - cut[..., None])
        src = np.zeros((B, W + 1), np.int64); np.put_along_axis(src, place.reshape(B, W), np.arange(W)[None, :], 1)
        p = ((ar * L[:, None]) >> LG)[..., None] + q * (1 + (u & (H - 1)))[..., None]
        p = np.where(p >= L[:, None, None], p - L[:, None, None], p)
        col = np.take_along_axis(src, p.reshape(B, W), 1)
        kid = np.take_along_axis(X, col[:, None, :], 2).reshape(N, 8, 16, G, C); nxt = np.empty_like(kid)
        for r in range(N):
            for d in range(N): nxt[d, :, :, r * M:(r + 1) * M] = kid[r, :, :, (d - r) % N::N]
        X = nxt.reshape(B, 16, W)
    return {"y": np.ascontiguousarray(X.reshape(N, 128, G, C)[..., :YC]).reshape(N, 128, G * YC).astype(np.float32).astype(BF)}

@@ -1,0 +1,500 @@
+from concourse.bass import DstId, RemoteDMATransfer
+from concourse.mybir import dt, AluOpType as A, AxisListType, ActivationFunctionType as F
+
+NV = 38
+NS = 64 - NV
+VCH = [2, 2, 2, 1, 1]
+SCH = [7, 3, 2, NS - 12, 0]
+SGR = [8, 12, NS - 20]
+RELU = (3, 4)
+RELAY = ((512, 512, 128), (512, 512, 128), (256, 256, 0))
+LAYS = (166, 166, 152)
+LAY0 = 64
+BIG = 16777216
+SC = NV * 8
+
+_F32 = [("wtf", 1), ("kmf", 24), ("thf", 8), ("mdg", 64), ("rst", 64), ("rcol", 1), ("qcol", 4), ("qj", 4), ("iq", 4), ("i64", 4), ("ib", 4), ("idf", 4), ("df", 4), ("defn", 4),
+        ("s16", 64), ("s32", 128), ("j64", 64), ("jp", 64), ("jm0", 64), ("jm1", 64), ("ej", 64), ("jj", 64), ("z64", 64), ("m0", 1), ("m1", 1), ("mm0", 4), ("mm1", 4),
+        ("c16", 256), ("kp", 64), ("th4", 512),
+        ("nx", 64), ("uf", 64), ("uk", 512), ("nk", 512), ("mk", 512), ("tm0", 2 * NV), ("tm1", NV),
+        ("ta", 4 * NS), ("tb", 2 * NS), ("bk", 64), ("t1", 64), ("bsc", 64), ("t0", 4), ("jf", 4), ("tt1", 4),
+        ("pm0", 128), ("px", 128), ("t2", 128), ("acs", 128), ("got", 4), ("cut", 4), ("pf", 4), ("z", 64), ("zc", 64), ("r1", 64), ("cr", 64), ("er", 64),
+        ("r2", 64), ("r3", 64), ("r4", 64), ("rl", 64), ("sl", 64), ("r8", 64), ("r12", 64), ("r16", 64), ("rl2", 64), ("sl2", 64), ("r32", 64), ("r48", 64),
+        ("kr", 66), ("rl3", 64), ("sl3", 64), ("lenl", 4), ("pm", 64), ("ps", 64), ("mlt", 64), ("ww", 64), ("ew", 64), ("vvv", 64), ("vv", 128),
+        ("dw", 256), ("ls", 256), ("hf", 64), ("hp", 64), ("h63", 64), ("lcol", 1), ("pp", 256), ("pq", 256), ("lp", 64), ("lw", 64), ("lq", 64), ("lm", 64), ("lsc", 64)]
+_I32 = [("wti", 1), ("kmi", 24), ("thi", 8), ("ia", 64), ("ibb", 64), ("icc", 1), ("id4", 4), ("ixo", 2 * NV), ("iu", 128), ("ui", 64), ("um", 64), ("uu", 64), ("vi", 64),
+        ("cp", 512), ("ci", 512), ("bi", 4), ("jb64", 4), ("ai", 4), ("pa", 4), ("oh", 4), ("pi", 64), ("pr", 64), ("tl4", 4), ("lsi", 256), ("lsa", 256),
+        ("h31", 64), ("si", 64), ("sp", 64)]
+_BF = [("xa", 4096), ("xb", 4096), ("xl0", 64), ("xl1", 64), ("xl2", 64), ("xp", 4096), ("kb0", 3072), ("kb1", 3072), ("kb2", 1536), ("yb", 2048),
+       ("xk0", 64), ("xk1", 64), ("ones", 128), ("bt", 128), ("blk", 128), ("wb", 128), ("sel", 144), ("sel2", 144), ("seln", 144), ("nb", 128),
+       ("u0", 128), ("u1", 128), ("b32", 128), ("b3t", 128), ("wm", 128), ("wm2", 128), ("lb0", 128), ("lb1", 128), ("lb2", 128), ("lb3", 128),
+       ("xr", 32 * NV), ("dv0", 32 * NV), ("dv1", 32 * NV), ("dv2", 32 * NV), ("av0", 32 * NV), ("av1", 32 * NV), ("av2", 32 * NV),
+       ("rv0", 32 * NV), ("rv1", 32 * NV), ("rv2", 32 * NV), ("as", 128 * NS),
+       ("pl", 8), ("cl", 8), ("cc0", 66), ("cc1", 66), ("cc2", 66), ("cc3", 66)]
+_U16 = [("xo", 2 * NV), ("of", 512), ("l1", 4), ("l4", 4), ("l16", 4), ("tl", 8), ("lay", 256), ("kl", 256), ("lx", 4)]
+_PS = ["pu", "pd0", "pd1", "pds", "pv", "plf", "ppos", "pw"]
+_OWN = ("xa", "xb", "xl0", "xl1", "xl2", "kb0", "kb1", "kb2", "yb", "xk0", "xk1", "wti", "kmi", "thi")
+SCRATCH = {}
+PLACE = {}
+for _l, _d, _b, _al in ((_F32, "float32", "ff", 8), (_I32, "int32", "ii", 8), (_BF, "bfloat16", "bb", 16), (_U16, "uint16", "uh", 16)):
+    _at = 0
+    for _n, _w in _l:
+        if _n in _OWN:
+            SCRATCH[_n] = ("sbuf", [128, _w], _d); PLACE[_n] = (_n, 0, _w)
+        else:
+            PLACE[_n] = (_b, _at, _w); _at += (_w + _al - 1) // _al * _al
+    SCRATCH[_b] = ("sbuf", [128, _at], _d)
+for _n in _PS:
+    SCRATCH[_n] = ("psum", [128, 512], "float32"); PLACE[_n] = (_n, 0, 512)
+SEMAPHORES = ["sv", "ss", "st", "sg", "lx0", "lx1", "lw", "lk", "lt", "xs1", "xs2", "stor"] + ["ra%d" % t for t in range(3)]
+SEMAPHORES += ["ar%d_%d" % (t, d) for t in range(3) for d in (1, 2, 3)] + ["tx%d" % t for t in range(3)] + ["ux%d" % t for t in range(2)]
+
+
+def rank_program(g, core, T, topo):
+    n_ranks = len(T.cores)
+
+    def helpers(rc):
+        return [c for c in topo.cores_of(rc) if topo.die(c) != topo.die(rc) and all(topo.may_write(c, d) for d in T.cores)]
+
+    def hop_engines(rc, hc, d):
+        off = topo.engines(rc, d)
+        return [e for e in topo.engines(rc, hc) if e not in off]
+
+    def width(t):
+        return 512 if t == 2 else 1024
+    rank = T.rank_of(core)
+    if rank is None:
+        for r, rc in enumerate(T.cores):
+            hs = helpers(rc)
+            if core not in hs: continue
+            k = hs.index(core)
+            for t in range(3):
+                if k >= len(RELAY[t]) or not RELAY[t][k]: continue
+                d = T.cores[(r + k + 1) % n_ranks]
+                rid, pid = topo.addr(d, core)
+                w = width(t); f = RELAY[t][k]; KB = "kb%d" % t; XN = "xa" if t == 1 else "xb" if t == 0 else "yb"
+                g.wait_ge(T.sem["ra%d" % t], len(hop_engines(rc, core, d)))
+                g.remote_dma(T[XN][:, r * w + w - f:r * w + w], T[KB][:, k * w + w - f:k * w + w], T.sem["ar%d_%d" % (t, k + 1)], T.sem["tx%d" % t], pid, rid, topo.mask(core, d))
+                g.wait_ge(T.sem["tx%d" % t], len(topo.engines(core, d)))
+        return
+    queue = {"v": g.vector, "s": g.scalar, "t": g.tensor, "g": g, "y": g.sync}
+    semname = {"v": "sv", "s": "ss", "t": "st", "g": "sg"}
+    count = {"v": 0, "s": 0, "t": 0, "g": 0}
+    value = {}
+    known = {q: {} for q in queue}
+    snap = {}
+    sent = [0, 0, 0]
+    log = {}
+
+    def D(n, lo=0, hi=None, st=1):
+        b, at, w = PLACE[n]
+        if hi is None: hi = w
+        hi = min(hi, w)
+        return (T[b][:, at + lo:at + hi] if st == 1 else T[b][:, at + lo:at + hi:st], [(n, lo, hi, st)])
+
+    def IND(win, off):
+        return (win[0].indirect(off[0]), win[1] + off[1])
+
+    def meet(a, b):
+        if a[0] >= b[1] or b[0] >= a[1]: return False
+        return not (a[2] == b[2] and a[2] > 1 and (a[0] - b[0]) % a[2] != 0)
+
+    def sync_for(q, outs, ins):
+        need = {}
+        for w, keys in ((True, outs), (False, ins)):
+            for (n, lo, hi, st) in keys:
+                ps = SCRATCH[PLACE[n][0]][0] == "psum"
+                for (src, w2, lo2, hi2, st2), k in log.get(n, {}).items():
+                    hit = (ps and src != q) or ((w or w2) and meet((lo, hi, st), (lo2, hi2, st2)))
+                    if hit and need.get(src, 0) < k: need[src] = k
+        for src, k in need.items():
+            wait(q, src, k)
+
+    def wait(q, src, k):
+        if known[q].get(src, 0) >= k: return
+        queue[q].wait_ge(T.sem[semname[src]], value[(src, k)])
+        for s2, k2 in list(snap[(src, k)].items()) + [(src, k)]:
+            if known[q].get(s2, 0) < k2: known[q][s2] = k2
+
+    def note(src, k, outs, ins):
+        for w, keys in ((True, outs), (False, ins)):
+            for (n, lo, hi, st) in keys:
+                log.setdefault(n, {})[(src, w, lo, hi, st)] = k
+
+    def done(q, ins_):
+        count[q] += 1
+        ins_.then_inc(T.sem[semname[q]], 1)
+        value[(q, count[q])] = count[q]
+        snap[(q, count[q])] = dict(known[q])
+        return count[q]
+
+    def source(name, sem, val, outs):
+        semname[name] = sem
+        value[(name, 1)] = val
+        snap[(name, 1)] = {}
+        note(name, 1, outs, [])
+
+    def col(x):
+        return (x[0], x[1]) if isinstance(x, tuple) else (x, [])
+
+    def run(q, o, i, make):
+        sync_for(q, o[1], i)
+        note(q, done(q, make()), o[1], i)
+
+    def vt(o, a, b, op): run("v", o, a[1] + b[1], lambda: g.vector.tensor_tensor(o[0], a[0], b[0], op))
+
+    def vs(o, a, s1, op0, s2=None, op1=None):
+        c1, k1 = col(s1); c2, k2 = col(s2)
+        if op1 is None: run("v", o, a[1] + k1, lambda: g.vector.tensor_scalar(o[0], a[0], c1, None, op0))
+        else: run("v", o, a[1] + k1 + k2, lambda: g.vector.tensor_scalar(o[0], a[0], c1, c2, op0, op1))
+
+    def vc(o, a): run("v", o, a[1], lambda: g.vector.tensor_copy(o[0], a[0]))
+
+    def vm(o, c): run("v", o, [], lambda: g.vector.memset(o[0], c))
+
+    def vscan(o, a, b, init, op0, op1):
+        c1, k1 = col(init)
+        run("v", o, a[1] + b[1] + k1, lambda: g.vector.tensor_tensor_scan(o[0], a[0], b[0], c1, op0, op1))
+
+    def vx(o, a): run("v", o, a[1], lambda: g.vector.transpose(o[0], a[0]))
+
+    def sa(o, a, f, bias=0.0, scale=1.0):
+        c1, k1 = col(bias); c2, k2 = col(scale)
+        run("s", o, a[1] + k1 + k2, lambda: g.scalar.activation(o[0], a[0], f, bias=c1, scale=c2))
+
+    def pe(o, *parts):
+        i = []
+        r = None
+        for p, pairs in enumerate(parts):
+            j = [k for a, b in pairs for k in a[1] + b[1]]
+            sync_for("t", o[1] if p == 0 else [], j)
+            i = i + j
+            for n, (a, b) in enumerate(pairs):
+                r = g.tensor.matmul(o[0], a[0], b[0], p == 0 and n == 0, p == len(parts) - 1 and n == len(pairs) - 1)
+        note("t", done("t", r), o[1], i)
+
+    def gi(o, pattern, base, cm):
+        if SCRATCH[PLACE[o[1][0][0]][0]][2] == "int32": run("g", o, [], lambda: g.iota(o[0], pattern, base, cm))
+        else: run("g", o, [], lambda: g.iota(o[0], pattern, base, cm, allow_small_or_imprecise_dtypes=True))
+
+    def gsel(o, a, pattern, op, base, cm): run("g", o, a[1], lambda: g.affine_select(o[0], a[0], pattern, op, 0.0, base, cm))
+
+    h = 2048
+    g.sync.dma_start(T.xa[:, 0:h], T.gen0[:, 0:h]).then_inc(T.sem.lx0, 16); source("Lx0", "lx0", 16, D("xa", 0, h)[1])
+    g.scalar.dma_start(T.wti[:], T.wt[:]).then_inc(T.sem.lw, 16); source("Lw", "lw", 16, D("wti")[1])
+    g.scalar.dma_start(T.kmi[:], T.km[:]).then_inc(T.sem.lk, 16); source("Lk", "lk", 16, D("kmi")[1])
+    g.sync.dma_start(T.xa[:, h:4096], T.gen0[:, h:4096]).then_inc(T.sem.lx1, 16); source("Lx1", "lx1", 16, D("xa", h, 4096)[1])
+    g.scalar.dma_start(T.thi[:], T.th[:]).then_inc(T.sem.lt, 16); source("Lt", "lt", 16, D("thi")[1])
+
+    vm(D("ones"), 1.0); vm(D("sel"), 0.0)
+    gi(D("z64"), [[0, 64]], 0, 0)
+    gsel(D("bt"), D("ones"), [[-16, 8], [0, 16]], A.is_ge, 0, 1)
+    gsel(D("blk"), D("bt"), [[16, 8], [0, 16]], A.is_ge, 15, -1)
+    gi(D("icc"), [[0, 1]], 0, 1); gi(D("ibb"), [[1, 64]], 0, 0); gi(D("ia"), [[1, 64]], 128, -1)
+    gi(D("ixo"), [[0, 2], [1, NV]], 0, 0)
+    gi(D("j64"), [[64, 64]], 0, 0); gi(D("iq"), [[16, 4]], 0, 0)
+    gi(D("id4"), [[0, 4]], 0, 64); gi(D("ib"), [[2048, 2], [0, 2]], 0, 0); gi(D("idf"), [[0, 2], [2048, 2]], 0, 0)
+    gi(D("iu"), [[1, 128]], 128, -1)
+    gsel(D("b3t"), D("ones"), [[-32, 4], [0, 32]], A.is_ge, 0, 1)
+    gsel(D("b32"), D("b3t"), [[32, 4], [0, 32]], A.is_ge, 31, -1)
+    gi(D("nb"), [[0, 128]], -131072, 0)
+    vc(D("wtf"), D("wti")); vc(D("kmf"), D("kmi")); vs(D("thf"), D("thi"), 4096.0, A.mult, float(-BIG), A.add)
+    vs(D("sel", 15, 143, 16), D("blk", 0, 128, 16), 4096.0, A.mult)
+    vs(D("wb"), D("blk"), D("wtf"), A.mult)
+    vs(D("pi", 0, 1), D("icc"), 15, A.bitwise_and); vs(D("pr", 0, 1), D("icc"), 4, A.logical_shift_right, 1, A.bitwise_and)
+    vc(D("rcol"), D("pi", 0, 1)); vc(D("m1"), D("pr", 0, 1))
+    vs(D("um"), D("ibb"), 15, A.bitwise_and); vs(D("ui"), D("ia"), 15, A.bitwise_and)
+    vs(D("rst"), D("um"), 0.0, A.not_equal); vs(D("mdg"), D("ui"), 0.0, A.is_equal)
+    vc(D("xo"), D("ixo"))
+    vs(D("bi"), D("id4"), 2047, A.bitwise_and); vs(D("ci", 0, 128), D("iu"), 15, A.bitwise_and)
+    vt(D("i64"), D("bi"), D("ib"), A.add); vt(D("df"), D("bi"), D("idf"), A.add); vs(D("wm"), D("ci", 0, 128), 0.0, A.is_equal)
+    vs(D("defn"), D("df"), -4096.0, A.add)
+    vm(D("s32"), float(-2 * BIG)); vm(D("s32", 0, 128, 32), 1.0)
+    vt(D("wm2"), D("wm"), D("b32"), A.mult)
+    vm(D("dw"), 0.0)
+    sa(D("sel2"), D("sel"), F.Copy, 0.0, 2.0); sa(D("seln"), D("sel"), F.Copy, 0.0, -1.0)
+    sa(D("m0"), D("m1"), F.Copy, 1.0, -1.0)
+    sa(D("mm1"), D("z64", 0, 4), F.Identity, D("m1")); sa(D("mm0"), D("z64", 0, 4), F.Identity, D("m0"))
+    sa(D("s16"), D("rst"), F.Copy, 1.0, float(-2 * BIG))
+    sa(D("jj"), D("j64"), F.Copy, 0.0, 1.0 / 4096); sa(D("ej"), D("j64"), F.Identity, D("rcol"))
+    sa(D("qcol"), D("iq"), F.Identity, D("rcol")); sa(D("qj"), D("qcol"), F.Copy, 0.0, 0.015625)
+    for m in range(8):
+        sa(D("th4", m * NV, m * NV + NV), D("z64", 0, NV), F.Identity, D("thf", m, m + 1))
+        sa(D("th4", SC + m, 512, 8), D("z64", 0, NS), F.Identity, D("thf", m, m + 1))
+    gsel(D("u0"), D("wm2"), [[0, 4], [1, 2], [0, 16]], A.is_equal, 0, 0)
+    gsel(D("u1"), D("wm2"), [[0, 4], [1, 2], [0, 16]], A.is_gt, 0, 0)
+    gi(D("kr"), [[0, 66]], 1000000, 0); gi(D("c16"), [[0, 256]], 16, 0)
+    gi(D("kp", 0, 48), [[1, 3], [4, 16]], 1, 0); gi(D("kp", 48, 64), [[4, 16]], 0, 0)
+    gi(D("jp"), [[64, 64]], 64, 0)
+    for b in range(2):
+        for a in range(4):
+            o = D("jm%d" % b); q = D("jp")
+            ot, oc = PLACE["jm%d" % b][:2]; qt, qc = PLACE["jp"][:2]
+            wait("g", "g", count["g"])
+            run("g", o, q[1], lambda: g.affine_select(T[ot][32 * a:32 * a + 32, oc:oc + 64], T[qt][32 * a:32 * a + 32, qc:qc + 64], [[1, 64]], A.is_gt, 0.0, -32 * b, -1))
+
+    for t in range(3):
+        last = t == 2
+        X = "xb" if t == 1 else "xa"
+        XL = "xl%d" % t
+
+        def hashes(lo, hi):
+            pe(D("pu", lo, hi), [(D("wb"), D(XL, lo, hi))])
+            vc(D("ui", lo, hi), D("pu", lo, hi)); vs(D("um", lo, hi), D("ui", lo, hi), 4095, A.bitwise_and)
+            vt(D("uu", lo, hi), D("um", lo, hi), D("um", lo, hi), A.mult); vs(D("vi", lo, hi), D("uu", lo, hi), 5, A.logical_shift_right)
+
+        def times(o, lo, hi, m):
+            k = D("kmf", t * 8 + m, t * 8 + m + 1)
+            if t or (lo == 0 and m > 1): sa(o, D("uf", lo, hi), F.Identity, 0.0, k)
+            else: vs(o, D("um", lo, hi), k, A.mult)
+
+        def lists(ms):
+            for m in ms: times(D("uk", m * NV, m * NV + NV), 0, NV, m)
+            for m in ms: vt(D("cp", m * NV, m * NV + NV), D("uk", m * NV, m * NV + NV), D("vi", 0, NV), A.add)
+            lo, hi = ms[0] * NV, ms[-1] * NV + NV
+            vs(D("ci", lo, hi), D("cp", lo, hi), 4095, A.bitwise_and); vc(D("of", lo, hi), D("ci", lo, hi))
+
+        def slists():
+            sa(D("nx", NV, 64), D(XL, NV, 64), F.Copy, 0.0, -1.0)
+            for m in range(8): times(D("uk", SC + m, 512, 8), NV, 64, m)
+            for m in range(8): vt(D("cp", SC + m, 512, 8), D("uk", SC + m, 512, 8), D("vi", NV, 64), A.add)
+            vs(D("ci", SC, 512), D("cp", SC, 512), 4095, A.bitwise_and); vc(D("of", SC, 512), D("ci", SC, 512))
+        if t == 0:
+            vc(D(XL), D(X, 63, 4096, 64))
+            sa(D("xr"), IND(D(XL), D("xo")), F.Copy)
+            hashes(0, 64)
+            lists([0, 1]); vc(D("uf"), D("um")); slists()
+        else:
+            hashes(0, 64)
+            vc(D("uf"), D("um"))
+            lists(list(range(8))); slists()
+            sa(D("xr"), IND(D(XL), D("xo")), F.Copy)
+        nq = 2 if last else 4
+
+        def strides():
+            vs(D("h31"), D("um"), 31, A.bitwise_and)
+            vs(D("hf"), D("h31"), 1.0, A.add)
+            for k in range(4): sa(D("hp", 16 * k, 16 * k + 16), D("hf", (k + 1) % 4, 64, 4), F.Copy)
+            for k in range(nq): sa(D("pw", k, 64 * nq, nq), D("hp"), F.Identity, 0.0, D("qcol", k, k + 1))
+            if not last: sa(D("h63"), D("hp"), F.Copy, 0.0, 63.0)
+        bank = ["pd0", "pd0", "pd1", "pd1", "pu"]
+        at = [0, 2 * NV, 0, 2 * NV, 0]
+        sbank = ["pds", "pds", "plf"]
+        scol = [0, 8 * SGR[0], 0]
+        m0 = [sum(VCH[:c]) for c in range(5)]
+        s0 = [sum(SGR[:c]) for c in range(4)]
+
+        def vgather(c):
+            n = 16 * VCH[c] * NV
+            dv = D("dv%d" % (c % 3), 0, n)
+            vt(dv, IND(D(X), D("of", m0[c] * NV, (m0[c] + VCH[c]) * NV)), D("xr", 0, n), A.subtract)
+            if c in RELU: vs(D("rv%d" % (c % 3), 0, n), dv, 0.0, A.max)
+
+        def sgather(c):
+            for i in range(sum(SCH[:c]), sum(SCH[:c + 1])):
+                sa(D("as", i * 128, i * 128 + 128), IND(D(X), D("of", SC + 8 * i, SC + 8 * i + 8)), F.Abs, D("nx", NV + i, NV + i + 1))
+            if c not in RELU: sa(D("av%d" % (c % 3), 0, 16 * VCH[c] * NV), D("dv%d" % (c % 3), 0, 16 * VCH[c] * NV), F.Abs)
+
+        def sums(s, b, lo, hi):
+            return [(D(s, 15 - r, 143 - r), D(b, lo + r, hi, 16)) for r in range(16)]
+
+        def vsums(c):
+            n = VCH[c] * NV
+            o = D(bank[c], at[c], at[c] + n)
+            e = c % 3
+            bias = [(D("nb"), D("ones", 0, n))]
+            if c in RELU: pe(o, bias + sums("seln", "dv%d" % e, 0, 16 * n), sums("sel2", "rv%d" % e, 0, 16 * n))
+            else: pe(o, bias + sums("sel", "av%d" % e, 0, 16 * n))
+
+        def ssums(q):
+            n = 8 * SGR[q]
+            pe(D(sbank[q], scol[q], scol[q] + n), [(D("nb"), D("ones", 0, n))] + sums("sel", "as", s0[q] * 128, s0[q + 1] * 128))
+
+        def posts(parts):
+            for P, b, lo, n in parts: vt(D("nk", lo, lo + n), D(P, b, b + n), D("ci", lo, lo + n), A.add)
+            for P, b, lo, n in parts: vt(D("pv", lo, lo + n), D(P, b, b + n), D("th4", lo, lo + n), A.is_lt)
+            for P, b, lo, n in parts: vt(D("mk", lo, lo + n), D("pv", lo, lo + n), D("nk", lo, lo + n), A.mult)
+
+        def smin(q):
+            lo, hi = SC + 8 * s0[q], SC + 8 * s0[q + 1]
+            a, b = s0[q], s0[q + 1]
+            yield vt(D("ta", 4 * a, 4 * b), D("mk", lo, hi, 2), D("mk", lo + 1, hi, 2), A.min)
+            yield vt(D("tb", 2 * a, 2 * b), D("ta", 4 * a, 4 * b, 2), D("ta", 4 * a + 1, 4 * b, 2), A.min)
+            yield vt(D("bk", NV + a, NV + b), D("tb", 2 * a, 2 * b, 2), D("tb", 2 * a + 1, 2 * b, 2), A.min)
+
+        def weave(*gs):
+            for _ in range(4):
+                for x in gs: next(x, None)
+        bv = D("bk", 0, NV)
+
+        def M(m, k=1): return D("mk", m * NV, (m + k) * NV)
+
+        def amin():
+            yield vt(D("tm0"), M(0, 2), M(2, 2), A.min)
+            yield vt(bv, D("tm0", 0, NV), D("tm0", NV, 2 * NV), A.min)
+
+        def bmin():
+            yield vt(D("tm0", 0, NV), M(4), M(5), A.min)
+            yield vt(D("tm1"), D("tm0", 0, NV), M(6), A.min)
+            yield vt(bv, bv, D("tm1"), A.min)
+        vgather(0)
+        if t == 0: lists(list(range(2, 8)))
+        sgather(0)
+        vgather(1); vsums(0); sgather(1); ssums(0)
+        vgather(2); vsums(1); sgather(2); vsums(2); sgather(3)
+        posts([("pd0", 0, 0, 4 * NV)]); weave(amin())
+        vgather(3); vsums(3); ssums(1)
+        vgather(4); vsums(4); ssums(2)
+        strides()
+        posts([("pd1", 0, 4 * NV, 3 * NV), ("pds", 0, SC, 8 * s0[2])]); weave(bmin(), smin(0), smin(1))
+        posts([("pu", 0, 7 * NV, NV), ("plf", 0, SC + 8 * s0[2], 8 * SGR[2])])
+        weave(smin(2), iter([vt(bv, bv, M(7), A.min)]))
+        vx(D("t1"), D("bk"))
+        vscan(D("bsc"), D("s16"), D("t1"), 0.0, A.max, A.min)
+        vc(D("bi"), D("bsc", 15, 64, 16)); vt(D("t0"), D("bsc", 15, 64, 16), D("i64"), A.add)
+        vs(D("jb64"), D("bi"), 4032, A.bitwise_and)
+        vt(D("tt1"), D("t0"), D("jb64"), A.subtract); vs(D("jf"), D("jb64"), 64.0, A.add)
+        for b in range(2):
+            for s in range(2):
+                c = 2 * b + s
+                vs(D("pm0", 64 * s, 64 * s + 64) if b == 0 else D("pv", 64 * s, 64 * s + 64), D("jm%d" % b), D("jf", c, c + 1), A.is_equal, D("tt1", c, c + 1), A.mult)
+        vt(D("px"), D("pm0"), D("pv", 0, 128), A.min)
+        vx(D("t2"), D("px"))
+        vscan(D("acs"), D("s32"), D("t2"), 0.0, A.max, A.min)
+        vt(D("ai"), D("acs", 31, 128, 32), D("defn"), A.min); sa(D("got"), D("acs", 31, 128, 32), F.Sign, 0.0, -1.0)
+        vs(D("pa"), D("ai"), 4032, A.bitwise_and, 6, A.logical_shift_right)
+        vs(D("oh"), D("ai"), 62, A.bitwise_and, 1, A.logical_shift_right)
+        vc(D("pf"), D("pa"))
+        for x in range(2): vt(D("pl", x, 8, 2), D("pa"), D("mm%d" % x), A.mult)
+        bs = (0, 2, 1, 3)
+        for c in range(4):
+            zo = D("z", 16 * c, 16 * c + 16); zi = D("pf", bs[c], bs[c] + 1)
+            if c < 2: sa(zo, D("z64", 0, 16), F.Identity, zi)
+            else: vs(zo, D("z64", 0, 16), zi, A.add)
+        pe(D("plf", 0, 4), [(D("u0"), D("pl", 0, 4)), (D("u1"), D("pl", 4, 8))])
+        vt(D("cut"), D("oh"), D("got"), A.add)
+        vx(D("r1"), D("z")); vc(D("l1"), D("plf", 0, 4))
+        L1 = D("l1"); L4 = D("l4"); L16 = D("l16")
+        for x in range(2): sa(D("cl", x, 8, 2), D("cut"), F.Identity, 0.0, D("m%d" % x))
+        for c in range(4): sa(D("zc", 16 * c, 16 * c + 16), D("z64", 0, 16), F.Identity, D("cut", bs[c], bs[c] + 1))
+        vc(D("r2"), IND(D("r1"), L1))
+        vc(D("r3"), IND(D("r2"), L1))
+        vt(D("rl"), IND(D("r3"), L1), D("mdg"), A.mult); sa(D("r4"), IND(D("r3"), L1), F.Copy)
+        vscan(D("sl"), D("rst"), D("rl"), 0.0, A.mult, A.add)
+        pe(D("plf", 4, 8), [(D("u0"), D("cl", 0, 4)), (D("u1"), D("cl", 4, 8))])
+        vx(D("cr"), D("zc"))
+        vc(L4, D("sl", 15, 64, 16))
+        sa(D("lenl"), D("plf", 4, 8), F.Copy, 64.0, -1.0)
+        for q in range(4): sa(D("lb%d" % q), D("blk"), F.Identity, 0.0, D("lenl", q, q + 1))
+        vc(D("r8"), IND(D("r4"), L4))
+        vt(D("er"), D("cr"), D("ej"), A.add)
+        vc(D("r12"), IND(D("r8"), L4))
+        vt(D("rl2"), IND(D("r12"), L4), D("mdg"), A.mult); sa(D("r16"), IND(D("r12"), L4), F.Copy)
+        vscan(D("sl2"), D("rst"), D("rl2"), 0.0, A.mult, A.add)
+        vc(L16, D("sl2", 15, 64, 16))
+        vc(D("r32"), IND(D("r16"), L16))
+        vc(D("r48"), IND(D("r32"), L16))
+        vt(D("rl3"), IND(D("r48"), L16), D("mdg"), A.mult)
+        vt(D("kr", 0, 64), IND(D("r48"), L16), D("jj"), A.add)
+        vscan(D("sl3"), D("rst"), D("rl3"), 0.0, A.mult, A.add)
+        for q in range(4): vs(D("cc%d" % q, 0, 65), D("kr", 0, 65), D("sl3", 16 * q + 15, 16 * q + 16), A.subtract, D("qj", q, q + 1), A.is_gt)
+        pe(D("ppos", 0, 65), [(D("lb%d" % q), D("cc%d" % q, 0, 65)) for q in range(4)])
+        vs(D("ww"), D("kr", 0, 64), 262144.0, A.mult); vt(D("ew"), D("er"), D("ww"), A.add)
+        vt(D("pm"), D("ppos", 0, 64), D("mdg"), A.mult)
+        vc(D("pi"), D("ppos", 0, 64))
+        vscan(D("ps"), D("rst"), D("pm"), 0.0, A.mult, A.add)
+        sa(D("lcol"), D("ppos", 64, 65), F.Copy)
+        vs(D("pr"), D("pi"), 15, A.bitwise_and)
+        vs(D("tl4"), D("ps", 15, 64, 16), 0.0625, A.mult, -0.46875, A.add)
+        vt(D("vvv"), D("ew"), D("pr"), A.subtract); vs(D("mlt"), D("pr"), D("rcol"), A.is_le)
+        vc(D("tl", 0, 4), D("tl4")); vs(D("tl", 4, 8), D("tl4"), 1.0, A.add)
+        vt(D("vv", 0, 64), D("vvv"), D("mlt"), A.mult); vs(D("vv", 64, 128), D("vvv"), 16.0, A.add)
+        vs(D("si"), D("kp"), D("lcol"), A.mult)
+        vc(IND(D("dw"), D("tl")), D("vv"))
+        vs(D("sp"), D("si"), 6, A.logical_shift_right)
+        vscan(D("ls", 0, LAY0), D("c16", 0, LAY0), D("dw", 0, LAY0), -1000.0, A.add, A.max)
+        vc(D("lsi", 0, LAY0), D("ls", 0, LAY0))
+        vscan(D("ls", LAY0, 256), D("c16", LAY0, 256), D("dw", LAY0, 256), D("ls", LAY0 - 1, LAY0), A.add, A.max)
+        vs(D("lsa", 0, LAY0), D("lsi", 0, LAY0), 4095, A.bitwise_and)
+        vc(D("lsi", LAY0, 256), D("ls", LAY0, 256))
+        vc(D("lay", 0, LAY0), D("lsa", 0, LAY0))
+        vs(D("lsa", LAY0, 256), D("lsi", LAY0, 256), 4095, A.bitwise_and)
+        vc(D("lay", LAY0, 256), D("lsa", LAY0, 256))
+        sa(D("xp", 0, 16 * LAY0), IND(D(X), D("lay", 0, LAY0)), F.Copy)
+        sa(D("xp", 16 * LAY0, 16 * LAYS[t]), IND(D(X), D("lay", LAY0, LAYS[t])), F.Copy)
+        if not last: vt(D("lp"), D("h63"), D("sp"), A.add)
+        for k in range(nq): vt(D("pp", k, 64 * nq, nq), D("pw", k, 64 * nq, nq), D("sp"), A.add)
+        if not last:
+            vs(D("lw"), D("lp"), D("lcol"), A.is_ge, D("lcol"), A.mult)
+        vs(D("pv", 0, 64 * nq), D("pp", 0, 64 * nq), D("lcol"), A.is_ge, D("lcol"), A.mult)
+        if not last: vt(D("lq"), D("lp"), D("lw"), A.subtract)
+        vt(D("pq", 0, 64 * nq), D("pp", 0, 64 * nq), D("pv", 0, 64 * nq), A.subtract)
+        if not last: vt(D("lm"), D("lq"), D("mdg"), A.mult)
+        vc(D("kl", 0, 64 * nq), D("pq", 0, 64 * nq))
+        if not last: vscan(D("lsc"), D("rst"), D("lm"), 0.0, A.mult, A.add)
+        vc(D("xp", 16 * LAYS[t], 4096), IND(D(X), D("lay", LAYS[t], 256)))
+        if not last: vc(D("lx"), D("lsc", 15, 64, 16))
+        w = width(t)
+        XN = "yb" if last else ("xa" if t == 1 else "xb")
+        KB = "kb%d" % t
+        if not last:
+            XK = "xk%d" % t; XLN = "xl%d" % (t + 1)
+            vc(D(XK), IND(D("xp"), D("lx")))
+            sync_for("g", [], D(XK, 0, 48)[1])
+            trs = []
+            for k in range(3):
+                d = T.cores[(rank + k + 1) % n_ranks]
+                rid, pid = topo.addr(d, core)
+                en = topo.engines(core, d)
+                mask = (1 << en[2 * k]) + (1 << en[2 * k + 1])
+                trs.append(RemoteDMATransfer(dst_ids=[DstId(rid=rid, pnc=pid)], dma_engine_mask=mask, remote_sem=T.sem["xs%d" % (t + 1)],
+                                             src=T[XK][:, 16 * k:16 * k + 16], dst=T[XLN][:, 16 * rank:16 * rank + 16]))
+            g.remote_dma_fused(trs, local_sem=T.sem["ux%d" % t])
+            for k in range(1, 4):
+                p = (rank - k) % n_ranks
+                source("XS%d" % (t + 1), "xs%d" % (t + 1), 6, D(XLN, 16 * p, 16 * p + 16)[1])
+        for k in range(4):
+            n = w // 32
+            if k < 3: oa = D(KB, k * w, k * w + w // 2); ob = D(KB, k * w + w // 2, k * w + w)
+            else: oa = D(XN, rank * w, rank * w + w // 2); ob = D(XN, rank * w + w // 2, rank * w + w)
+            if k == 3 and not last: sa(oa, IND(D("xp"), D("kl", 2 * k * n, 2 * k * n + n)), F.Copy)
+            else: vc(oa, IND(D("xp"), D("kl", 2 * k * n, 2 * k * n + n)))
+            sa(ob, IND(D("xp"), D("kl", 2 * k * n + n, 2 * k * n + 2 * n)), F.Copy)
+            if k < 3:
+                d = T.cores[(rank + k + 1) % n_ranks]
+                rid, pid = topo.addr(d, core)
+                sync_for("g", [], D(KB, k * w, k * w + w)[1])
+                ar = T.sem["ar%d_%d" % (t, k + 1)]; tx = T.sem["tx%d" % t]
+                mask = topo.mask(core, d)
+                f = RELAY[t][k]
+                m = k * w + w - f
+                if f:
+                    hc = helpers(core)[k]
+                    hrid, hpid = topo.addr(hc, core)
+                    he = hop_engines(core, hc, d)
+                    hop = RemoteDMATransfer(dst_ids=[DstId(rid=hrid, pnc=hpid)], dma_engine_mask=sum(1 << e for e in he), remote_sem=T.sem["ra%d" % t], src=T[KB][:, m:k * w + w], dst=T[KB][:, m:k * w + w])
+                    on = RemoteDMATransfer(dst_ids=[DstId(rid=rid, pnc=pid)], dma_engine_mask=mask, remote_sem=ar, src=T[KB][:, k * w:m], dst=T[XN][:, rank * w:rank * w + w - f])
+                    for trs in ([[hop, on]] if 2 * f == w else [[hop], [on]]): g.remote_dma_fused(trs, local_sem=tx)
+                    sent[t] += len(he)
+                else:
+                    g.remote_dma(T[XN][:, rank * w:rank * w + w], T[KB][:, k * w:k * w + w], ar, tx, pid, rid, mask)
+                sent[t] += len(topo.engines(core, d))
+        if not last:
+            vc(D(XLN, 16 * rank, 16 * rank + 16), D(XK, 48, 64))
+            vm(D("dw"), 0.0)
+        for k in range(1, 4):
+            p = (rank - k) % n_ranks
+            cnt = len(topo.engines(T.cores[p], core))
+            if RELAY[t][k - 1]: cnt += len(topo.engines(helpers(T.cores[p])[k - 1], core))
+            source("AR%d_%d" % (t, k), "ar%d_%d" % (t, k), cnt, D(XN, p * w, p * w + w)[1])
+
+    for k in range(4):
+        p = (rank - k) % n_ranks
+        sync_for("y", [], D("yb", p * 512, p * 512 + 512)[1])
+        g.sync.dma_start(T.y[:, p * 512:p * 512 + 512], T.yb[:, p * 512:p * 512 + 512]).then_inc(T.sem.stor, 16)
+    g.sync.wait_ge(T.sem.stor, 64)
+    for t in range(3):
+        g.wait_ge(T.sem["tx%d" % t], sent[t])
+        if t < 2: g.wait_ge(T.sem["ux%d" % t], 6)
+    for q in ("v", "s", "t", "g"):
+        wait("g", q, count[q])

@@ -1,37 +1,36 @@
 from concourse.bass import DstId, RemoteDMATransfer
 from concourse.mybir import dt, AluOpType as A, AxisListType, ActivationFunctionType as F
 
-NV = 38
+NV = 32
 NS = 64 - NV
-VCH = [2, 2, 2, 1, 1]
-SCH = [7, 3, 2, NS - 12, 0]
-SGR = [8, 12, NS - 20]
-RELU = (3, 4)
+SCH = [8, 6, 6, NS - 20]
+SGR = [12, 12, NS - 24]
+ABS = (0, 1)
+WIDTH = (1024, 1024, 512)
 RELAY = ((512, 512, 128), (512, 512, 128), (256, 256, 0))
-LAYS = (166, 166, 152)
+LAYS = (144, 144, 144)
 LAY0 = 64
 BIG = 16777216
 SC = NV * 8
 
 _F32 = [("wtf", 1), ("kmf", 24), ("thf", 8), ("mdg", 64), ("rst", 64), ("rcol", 1), ("qcol", 4), ("qj", 4), ("iq", 4), ("i64", 4), ("ib", 4), ("idf", 4), ("df", 4), ("defn", 4),
-        ("s16", 64), ("s32", 128), ("j64", 64), ("jp", 64), ("jm0", 64), ("jm1", 64), ("ej", 64), ("jj", 64), ("z64", 64), ("m0", 1), ("m1", 1), ("mm0", 4), ("mm1", 4),
+        ("s16", 64), ("s32", 128), ("s8", 8 * NS), ("j64", 64), ("jp", 64), ("jm0", 64), ("jm1", 64), ("ej", 64), ("jj", 64), ("z64", 64), ("m0", 1), ("m1", 1), ("mm0", 4), ("mm1", 4),
         ("c16", 256), ("kp", 64), ("th4", 512),
-        ("nx", 64), ("uf", 64), ("uk", 512), ("nk", 512), ("mk", 512), ("tm0", 2 * NV), ("tm1", NV),
-        ("ta", 4 * NS), ("tb", 2 * NS), ("bk", 64), ("t1", 64), ("bsc", 64), ("t0", 4), ("jf", 4), ("tt1", 4),
+        ("nx", 64), ("uf", 64), ("uk", 512), ("nk", 512), ("mk", 4 * NV), ("tm0", 2 * NV), ("sm", 8 * NS),
+        ("bk", 64), ("t1", 64), ("bsc", 64), ("t0", 4), ("jf", 4), ("tt1", 4),
         ("pm0", 128), ("px", 128), ("t2", 128), ("acs", 128), ("got", 4), ("cut", 4), ("pf", 4), ("z", 64), ("zc", 64), ("r1", 64), ("cr", 64), ("er", 64),
         ("r2", 64), ("r3", 64), ("r4", 64), ("rl", 64), ("sl", 64), ("r8", 64), ("r12", 64), ("r16", 64), ("rl2", 64), ("sl2", 64), ("r32", 64), ("r48", 64),
-        ("kr", 66), ("rl3", 64), ("sl3", 64), ("lenl", 4), ("pm", 64), ("ps", 64), ("mlt", 64), ("ww", 64), ("ew", 64), ("vvv", 64), ("vv", 128),
-        ("dw", 256), ("ls", 256), ("hf", 64), ("hp", 64), ("h63", 64), ("lcol", 1), ("pp", 256), ("pq", 256), ("lp", 64), ("lw", 64), ("lq", 64), ("lm", 64), ("lsc", 64)]
-_I32 = [("wti", 1), ("kmi", 24), ("thi", 8), ("ia", 64), ("ibb", 64), ("icc", 1), ("id4", 4), ("ixo", 2 * NV), ("iu", 128), ("ui", 64), ("um", 64), ("uu", 64), ("vi", 64),
+        ("kr", 64), ("rl3", 64), ("sl3", 64), ("lenl", 4), ("pm", 64), ("ps", 64), ("mlt", 64), ("ww", 64), ("ew", 64), ("vvv", 64), ("vv", 128),
+        ("dw", 256), ("ls", 256), ("hf", 64), ("hp", 64), ("lcol", 1), ("l64", 1), ("l8k", 1), ("pp", 320), ("wa", 320), ("pq", 320), ("lm", 64), ("lsc", 64)]
+_I32 = [("wti", 1), ("kmi", 24), ("thi", 8), ("ia", 64), ("ibb", 64), ("icc", 1), ("id4", 4), ("ixo", NV), ("iu", 128), ("ui", 64), ("um", 64), ("uu", 64), ("vi", 64),
         ("cp", 512), ("ci", 512), ("bi", 4), ("jb64", 4), ("ai", 4), ("pa", 4), ("oh", 4), ("pi", 64), ("pr", 64), ("tl4", 4), ("lsi", 256), ("lsa", 256),
-        ("h31", 64), ("si", 64), ("sp", 64)]
+        ("h31", 64), ("sp", 64)]
 _BF = [("xa", 4096), ("xb", 4096), ("xl0", 64), ("xl1", 64), ("xl2", 64), ("xp", 4096), ("kb0", 3072), ("kb1", 3072), ("kb2", 1536), ("yb", 2048),
        ("xk0", 64), ("xk1", 64), ("ones", 128), ("bt", 128), ("blk", 128), ("wb", 128), ("sel", 144), ("sel2", 144), ("seln", 144), ("nb", 128),
        ("u0", 128), ("u1", 128), ("b32", 128), ("b3t", 128), ("wm", 128), ("wm2", 128), ("lb0", 128), ("lb1", 128), ("lb2", 128), ("lb3", 128),
-       ("xr", 32 * NV), ("dv0", 32 * NV), ("dv1", 32 * NV), ("dv2", 32 * NV), ("av0", 32 * NV), ("av1", 32 * NV), ("av2", 32 * NV),
-       ("rv0", 32 * NV), ("rv1", 32 * NV), ("rv2", 32 * NV), ("as", 128 * NS),
-       ("pl", 8), ("cl", 8), ("cc0", 66), ("cc1", 66), ("cc2", 66), ("cc3", 66)]
-_U16 = [("xo", 2 * NV), ("of", 512), ("l1", 4), ("l4", 4), ("l16", 4), ("tl", 8), ("lay", 256), ("kl", 256), ("lx", 4)]
+       ("xr", 16 * NV), ("dv", 128 * NV), ("av", 128 * NV), ("as", 128 * NS),
+       ("pl", 8), ("cl", 8), ("lenb", 4), ("cc0", 64), ("cc1", 64), ("cc2", 64), ("cc3", 64)]
+_U16 = [("xo", NV), ("of", 512), ("l1", 4), ("l4", 4), ("l16", 4), ("tl", 8), ("lay", 256), ("kl", 256), ("lx", 4)]
 _PS = ["pu", "pd0", "pd1", "pds", "pv", "plf", "ppos", "pw"]
 _OWN = ("xa", "xb", "xl0", "xl1", "xl2", "kb0", "kb1", "kb2", "yb", "xk0", "xk1", "wti", "kmi", "thi")
 SCRATCH = {}
@@ -46,12 +45,13 @@ for _l, _d, _b, _al in ((_F32, "float32", "ff", 8), (_I32, "int32", "ii", 8), (_
     SCRATCH[_b] = ("sbuf", [128, _at], _d)
 for _n in _PS:
     SCRATCH[_n] = ("psum", [128, 512], "float32"); PLACE[_n] = (_n, 0, 512)
-SEMAPHORES = ["sv", "ss", "st", "sg", "lx0", "lx1", "lw", "lk", "lt", "xs1", "xs2", "stor"] + ["ra%d" % t for t in range(3)]
-SEMAPHORES += ["ar%d_%d" % (t, d) for t in range(3) for d in (1, 2, 3)] + ["tx%d" % t for t in range(3)] + ["ux%d" % t for t in range(2)]
+SEMAPHORES = ["sv", "ss", "st", "sg", "lw", "lk", "lt", "lx0", "lx1", "xs1", "xs2", "stor", "tx", "ra0", "ra1", "ra2"]
+SEMAPHORES += ["ar%d_%d" % (t, k) for t in range(3) for k in range(3)]
 
 
 def rank_program(g, core, T, topo):
     n_ranks = len(T.cores)
+    SRC = ("kb0", "kb1", "kb2"); DST = ("xb", "xa", "yb")
 
     def helpers(rc):
         return [c for c in topo.cores_of(rc) if topo.die(c) != topo.die(rc) and all(topo.may_write(c, d) for d in T.cores)]
@@ -59,23 +59,22 @@ def rank_program(g, core, T, topo):
     def hop_engines(rc, hc, d):
         off = topo.engines(rc, d)
         return [e for e in topo.engines(rc, hc) if e not in off]
-
-    def width(t):
-        return 512 if t == 2 else 1024
     rank = T.rank_of(core)
     if rank is None:
         for r, rc in enumerate(T.cores):
             hs = helpers(rc)
             if core not in hs: continue
             k = hs.index(core)
+            n = 0
             for t in range(3):
                 if k >= len(RELAY[t]) or not RELAY[t][k]: continue
                 d = T.cores[(r + k + 1) % n_ranks]
                 rid, pid = topo.addr(d, core)
-                w = width(t); f = RELAY[t][k]; KB = "kb%d" % t; XN = "xa" if t == 1 else "xb" if t == 0 else "yb"
+                w = WIDTH[t]; f = RELAY[t][k]
                 g.wait_ge(T.sem["ra%d" % t], len(hop_engines(rc, core, d)))
-                g.remote_dma(T[XN][:, r * w + w - f:r * w + w], T[KB][:, k * w + w - f:k * w + w], T.sem["ar%d_%d" % (t, k + 1)], T.sem["tx%d" % t], pid, rid, topo.mask(core, d))
-                g.wait_ge(T.sem["tx%d" % t], len(topo.engines(core, d)))
+                g.remote_dma(T[DST[t]][:, r * w + w - f:r * w + w], T[SRC[t]][:, k * w + w - f:k * w + w], T.sem["ar%d_%d" % (t, k)], T.sem.tx, pid, rid, topo.mask(core, d))
+                n += len(topo.engines(core, d))
+                g.wait_ge(T.sem.tx, n)
         return
     queue = {"v": g.vector, "s": g.scalar, "t": g.tensor, "g": g, "y": g.sync}
     semname = {"v": "sv", "s": "ss", "t": "st", "g": "sg"}
@@ -83,14 +82,14 @@ def rank_program(g, core, T, topo):
     value = {}
     known = {q: {} for q in queue}
     snap = {}
-    sent = [0, 0, 0]
+    sent = [0]
     log = {}
 
-    def D(n, lo=0, hi=None, st=1):
+    def D(n, lo=0, hi=None, st=1, p=(0, 128)):
         b, at, w = PLACE[n]
         if hi is None: hi = w
         hi = min(hi, w)
-        return (T[b][:, at + lo:at + hi] if st == 1 else T[b][:, at + lo:at + hi:st], [(n, lo, hi, st)])
+        return (T[b][p[0]:p[1], at + lo:at + hi] if st == 1 else T[b][p[0]:p[1], at + lo:at + hi:st], [(n, lo, hi, st)])
 
     def IND(win, off):
         return (win[0].indirect(off[0]), win[1] + off[1])
@@ -179,39 +178,66 @@ def rank_program(g, core, T, topo):
 
     def gsel(o, a, pattern, op, base, cm): run("g", o, a[1], lambda: g.affine_select(o[0], a[0], pattern, op, 0.0, base, cm))
 
-    h = 2048
-    g.sync.dma_start(T.xa[:, 0:h], T.gen0[:, 0:h]).then_inc(T.sem.lx0, 16); source("Lx0", "lx0", 16, D("xa", 0, h)[1])
-    g.scalar.dma_start(T.wti[:], T.wt[:]).then_inc(T.sem.lw, 16); source("Lw", "lw", 16, D("wti")[1])
-    g.scalar.dma_start(T.kmi[:], T.km[:]).then_inc(T.sem.lk, 16); source("Lk", "lk", 16, D("kmi")[1])
-    g.sync.dma_start(T.xa[:, h:4096], T.gen0[:, h:4096]).then_inc(T.sem.lx1, 16); source("Lx1", "lx1", 16, D("xa", h, 4096)[1])
-    g.scalar.dma_start(T.thi[:], T.th[:]).then_inc(T.sem.lt, 16); source("Lt", "lt", 16, D("thi")[1])
+    def load(q, sem, o, src):
+        queue[q].dma_start(o[0], src).then_inc(T.sem[sem], 16)
+        source(sem, sem, 16, o[1])
+
+    def send(t, k):
+        d = T.cores[(rank + k + 1) % n_ranks]
+        rid, pid = topo.addr(d, core)
+        w = WIDTH[t]; f = RELAY[t][k]; m = k * w + w - f; at = rank * w
+        S = T[SRC[t]]; ar = T.sem["ar%d_%d" % (t, k)]
+        sync_for("g", [], D(SRC[t], k * w, k * w + w)[1])
+        on = RemoteDMATransfer(dst_ids=[DstId(rid=rid, pnc=pid)], dma_engine_mask=topo.mask(core, d), remote_sem=ar, src=S[:, k * w:m], dst=T[DST[t]][:, at:at + w - f])
+        calls = [[on]]
+        if f:
+            hc = helpers(core)[k]
+            hrid, hpid = topo.addr(hc, core)
+            he = hop_engines(core, hc, d)
+            hop = RemoteDMATransfer(dst_ids=[DstId(rid=hrid, pnc=hpid)], dma_engine_mask=sum(1 << e for e in he), remote_sem=T.sem["ra%d" % t], src=S[:, m:k * w + w], dst=S[:, m:k * w + w])
+            calls = [[hop, on]] if 2 * f == w else [[hop], [on]]
+            sent[0] += len(he)
+        for trs in calls: g.remote_dma_fused(trs, local_sem=T.sem.tx)
+        sent[0] += len(topo.engines(core, d))
+
+    def arrival(t, k):
+        p = (rank - k - 1) % n_ranks
+        cnt = len(topo.engines(T.cores[p], core))
+        if RELAY[t][k]: cnt += len(topo.engines(helpers(T.cores[p])[k], core))
+        source("AR%d_%d" % (t, k), "ar%d_%d" % (t, k), cnt, D(DST[t], p * WIDTH[t], (p + 1) * WIDTH[t])[1])
+        return p
+
+    load("y", "lx0", D("xa", 0, 2048), T.gen0[:, 0:2048])
+    load("s", "lw", D("wti"), T.wt[:]); load("s", "lk", D("kmi"), T.km[:])
+    load("y", "lx1", D("xa", 2048, 4096), T.gen0[:, 2048:4096])
+    load("s", "lt", D("thi"), T.th[:])
 
     vm(D("ones"), 1.0); vm(D("sel"), 0.0)
     gi(D("z64"), [[0, 64]], 0, 0)
     gsel(D("bt"), D("ones"), [[-16, 8], [0, 16]], A.is_ge, 0, 1)
     gsel(D("blk"), D("bt"), [[16, 8], [0, 16]], A.is_ge, 15, -1)
     gi(D("icc"), [[0, 1]], 0, 1); gi(D("ibb"), [[1, 64]], 0, 0); gi(D("ia"), [[1, 64]], 128, -1)
-    gi(D("ixo"), [[0, 2], [1, NV]], 0, 0)
+    gi(D("ixo"), [[1, NV]], 0, 0)
     gi(D("j64"), [[64, 64]], 0, 0); gi(D("iq"), [[16, 4]], 0, 0)
     gi(D("id4"), [[0, 4]], 0, 64); gi(D("ib"), [[2048, 2], [0, 2]], 0, 0); gi(D("idf"), [[0, 2], [2048, 2]], 0, 0)
     gi(D("iu"), [[1, 128]], 128, -1)
     gsel(D("b3t"), D("ones"), [[-32, 4], [0, 32]], A.is_ge, 0, 1)
     gsel(D("b32"), D("b3t"), [[32, 4], [0, 32]], A.is_ge, 31, -1)
     gi(D("nb"), [[0, 128]], -131072, 0)
-    vc(D("wtf"), D("wti")); vc(D("kmf"), D("kmi")); vs(D("thf"), D("thi"), 4096.0, A.mult, float(-BIG), A.add)
+    vm(D("s32"), float(-2 * BIG)); vm(D("s8"), float(-2 * BIG)); vm(D("s32", 0, 128, 32), 1.0); vm(D("s8", 0, 8 * NS, 8), 1.0)
     vs(D("sel", 15, 143, 16), D("blk", 0, 128, 16), 4096.0, A.mult)
-    vs(D("wb"), D("blk"), D("wtf"), A.mult)
     vs(D("pi", 0, 1), D("icc"), 15, A.bitwise_and); vs(D("pr", 0, 1), D("icc"), 4, A.logical_shift_right, 1, A.bitwise_and)
     vc(D("rcol"), D("pi", 0, 1)); vc(D("m1"), D("pr", 0, 1))
     vs(D("um"), D("ibb"), 15, A.bitwise_and); vs(D("ui"), D("ia"), 15, A.bitwise_and)
     vs(D("rst"), D("um"), 0.0, A.not_equal); vs(D("mdg"), D("ui"), 0.0, A.is_equal)
     vc(D("xo"), D("ixo"))
+    vc(D("wtf"), D("wti")); vc(D("kmf"), D("kmi"))
+    vs(D("wb"), D("blk"), D("wtf"), A.mult)
     vs(D("bi"), D("id4"), 2047, A.bitwise_and); vs(D("ci", 0, 128), D("iu"), 15, A.bitwise_and)
     vt(D("i64"), D("bi"), D("ib"), A.add); vt(D("df"), D("bi"), D("idf"), A.add); vs(D("wm"), D("ci", 0, 128), 0.0, A.is_equal)
     vs(D("defn"), D("df"), -4096.0, A.add)
-    vm(D("s32"), float(-2 * BIG)); vm(D("s32", 0, 128, 32), 1.0)
+    vs(D("thf"), D("thi"), 4096.0, A.mult, float(-BIG), A.add)
     vt(D("wm2"), D("wm"), D("b32"), A.mult)
-    vm(D("dw"), 0.0)
     sa(D("sel2"), D("sel"), F.Copy, 0.0, 2.0); sa(D("seln"), D("sel"), F.Copy, 0.0, -1.0)
     sa(D("m0"), D("m1"), F.Copy, 1.0, -1.0)
     sa(D("mm1"), D("z64", 0, 4), F.Identity, D("m1")); sa(D("mm0"), D("z64", 0, 4), F.Identity, D("m0"))
@@ -223,137 +249,119 @@ def rank_program(g, core, T, topo):
         sa(D("th4", SC + m, 512, 8), D("z64", 0, NS), F.Identity, D("thf", m, m + 1))
     gsel(D("u0"), D("wm2"), [[0, 4], [1, 2], [0, 16]], A.is_equal, 0, 0)
     gsel(D("u1"), D("wm2"), [[0, 4], [1, 2], [0, 16]], A.is_gt, 0, 0)
-    gi(D("kr"), [[0, 66]], 1000000, 0); gi(D("c16"), [[0, 256]], 16, 0)
+    gi(D("c16"), [[0, 256]], 16, 0)
     gi(D("kp", 0, 48), [[1, 3], [4, 16]], 1, 0); gi(D("kp", 48, 64), [[4, 16]], 0, 0)
     gi(D("jp"), [[64, 64]], 64, 0)
     for b in range(2):
         for a in range(4):
-            o = D("jm%d" % b); q = D("jp")
-            ot, oc = PLACE["jm%d" % b][:2]; qt, qc = PLACE["jp"][:2]
             wait("g", "g", count["g"])
-            run("g", o, q[1], lambda: g.affine_select(T[ot][32 * a:32 * a + 32, oc:oc + 64], T[qt][32 * a:32 * a + 32, qc:qc + 64], [[1, 64]], A.is_gt, 0.0, -32 * b, -1))
+            gsel(D("jm%d" % b, p=(32 * a, 32 * a + 32)), D("jp", p=(32 * a, 32 * a + 32)), [[1, 64]], A.is_gt, -32 * b, -1)
 
     for t in range(3):
         last = t == 2
         X = "xb" if t == 1 else "xa"
         XL = "xl%d" % t
 
-        def hashes(lo, hi):
-            pe(D("pu", lo, hi), [(D("wb"), D(XL, lo, hi))])
-            vc(D("ui", lo, hi), D("pu", lo, hi)); vs(D("um", lo, hi), D("ui", lo, hi), 4095, A.bitwise_and)
-            vt(D("uu", lo, hi), D("um", lo, hi), D("um", lo, hi), A.mult); vs(D("vi", lo, hi), D("uu", lo, hi), 5, A.logical_shift_right)
-
         def times(o, lo, hi, m):
             k = D("kmf", t * 8 + m, t * 8 + m + 1)
             if t or (lo == 0 and m > 1): sa(o, D("uf", lo, hi), F.Identity, 0.0, k)
             else: vs(o, D("um", lo, hi), k, A.mult)
 
+        def offsets(lo, hi):
+            vs(D("ci", lo, hi), D("cp", lo, hi), 4095, A.bitwise_and); vc(D("of", lo, hi), D("ci", lo, hi))
+
         def lists(ms):
             for m in ms: times(D("uk", m * NV, m * NV + NV), 0, NV, m)
             for m in ms: vt(D("cp", m * NV, m * NV + NV), D("uk", m * NV, m * NV + NV), D("vi", 0, NV), A.add)
-            lo, hi = ms[0] * NV, ms[-1] * NV + NV
-            vs(D("ci", lo, hi), D("cp", lo, hi), 4095, A.bitwise_and); vc(D("of", lo, hi), D("ci", lo, hi))
+            offsets(ms[0] * NV, ms[-1] * NV + NV)
 
         def slists():
             sa(D("nx", NV, 64), D(XL, NV, 64), F.Copy, 0.0, -1.0)
             for m in range(8): times(D("uk", SC + m, 512, 8), NV, 64, m)
             for m in range(8): vt(D("cp", SC + m, 512, 8), D("uk", SC + m, 512, 8), D("vi", NV, 64), A.add)
-            vs(D("ci", SC, 512), D("cp", SC, 512), 4095, A.bitwise_and); vc(D("of", SC, 512), D("ci", SC, 512))
+            offsets(SC, 512)
+        if t == 0: vc(D(XL), D(X, 63, 4096, 64))
+        sa(D("xr"), IND(D(XL), D("xo")), F.Copy)
+        pe(D("pu", 0, 64), [(D("wb"), D(XL))])
+        vc(D("ui"), D("pu", 0, 64)); vs(D("um"), D("ui"), 4095, A.bitwise_and)
+        if t: vc(D("uf"), D("um"))
+        vt(D("uu"), D("um"), D("um"), A.mult); vs(D("vi"), D("uu"), 5, A.logical_shift_right)
         if t == 0:
-            vc(D(XL), D(X, 63, 4096, 64))
-            sa(D("xr"), IND(D(XL), D("xo")), F.Copy)
-            hashes(0, 64)
             lists([0, 1]); vc(D("uf"), D("um")); slists()
         else:
-            hashes(0, 64)
-            vc(D("uf"), D("um"))
             lists(list(range(8))); slists()
-            sa(D("xr"), IND(D(XL), D("xo")), F.Copy)
         nq = 2 if last else 4
+        nk_ = 64 * nq
+        np_ = nk_ if last else nk_ + 64
 
         def strides():
             vs(D("h31"), D("um"), 31, A.bitwise_and)
             vs(D("hf"), D("h31"), 1.0, A.add)
+
+        def steps():
             for k in range(4): sa(D("hp", 16 * k, 16 * k + 16), D("hf", (k + 1) % 4, 64, 4), F.Copy)
-            for k in range(nq): sa(D("pw", k, 64 * nq, nq), D("hp"), F.Identity, 0.0, D("qcol", k, k + 1))
-            if not last: sa(D("h63"), D("hp"), F.Copy, 0.0, 63.0)
-        bank = ["pd0", "pd0", "pd1", "pd1", "pu"]
-        at = [0, 2 * NV, 0, 2 * NV, 0]
+            for k in range(nq): sa(D("pw", k, nk_, nq), D("hp"), F.Identity, 0.0, D("qcol", k, k + 1))
+            if not last: sa(D("pw", nk_, np_), D("hp"), F.Copy, 0.0, 63.0)
+        n1 = 16 * NV
+        bank = ["pd0", "pd0", "pd1", "pu"]
+        at = [0, 2 * NV, 0, 0]
         sbank = ["pds", "pds", "plf"]
         scol = [0, 8 * SGR[0], 0]
-        m0 = [sum(VCH[:c]) for c in range(5)]
         s0 = [sum(SGR[:c]) for c in range(4)]
 
         def vgather(c):
-            n = 16 * VCH[c] * NV
-            dv = D("dv%d" % (c % 3), 0, n)
-            vt(dv, IND(D(X), D("of", m0[c] * NV, (m0[c] + VCH[c]) * NV)), D("xr", 0, n), A.subtract)
-            if c in RELU: vs(D("rv%d" % (c % 3), 0, n), dv, 0.0, A.max)
+            for m in (2 * c, 2 * c + 1): vt(D("dv", m * n1, m * n1 + n1), IND(D(X), D("of", m * NV, m * NV + NV)), D("xr"), A.subtract)
+            if c not in ABS: vs(D("av", 2 * c * n1, 2 * c * n1 + 2 * n1), D("dv", 2 * c * n1, 2 * c * n1 + 2 * n1), 0.0, A.max)
 
         def sgather(c):
             for i in range(sum(SCH[:c]), sum(SCH[:c + 1])):
                 sa(D("as", i * 128, i * 128 + 128), IND(D(X), D("of", SC + 8 * i, SC + 8 * i + 8)), F.Abs, D("nx", NV + i, NV + i + 1))
-            if c not in RELU: sa(D("av%d" % (c % 3), 0, 16 * VCH[c] * NV), D("dv%d" % (c % 3), 0, 16 * VCH[c] * NV), F.Abs)
+            if c in ABS: sa(D("av", 2 * c * n1, 2 * c * n1 + 2 * n1), D("dv", 2 * c * n1, 2 * c * n1 + 2 * n1), F.Abs)
 
         def sums(s, b, lo, hi):
             return [(D(s, 15 - r, 143 - r), D(b, lo + r, hi, 16)) for r in range(16)]
 
         def vsums(c):
-            n = VCH[c] * NV
+            n = 2 * NV; lo = 2 * c * n1; hi = lo + 2 * n1
             o = D(bank[c], at[c], at[c] + n)
-            e = c % 3
             bias = [(D("nb"), D("ones", 0, n))]
-            if c in RELU: pe(o, bias + sums("seln", "dv%d" % e, 0, 16 * n), sums("sel2", "rv%d" % e, 0, 16 * n))
-            else: pe(o, bias + sums("sel", "av%d" % e, 0, 16 * n))
+            if c in ABS: pe(o, bias + sums("sel", "av", lo, hi))
+            else: pe(o, bias + sums("seln", "dv", lo, hi), sums("sel2", "av", lo, hi))
 
         def ssums(q):
             n = 8 * SGR[q]
             pe(D(sbank[q], scol[q], scol[q] + n), [(D("nb"), D("ones", 0, n))] + sums("sel", "as", s0[q] * 128, s0[q + 1] * 128))
 
         def posts(parts):
-            for P, b, lo, n in parts: vt(D("nk", lo, lo + n), D(P, b, b + n), D("ci", lo, lo + n), A.add)
-            for P, b, lo, n in parts: vt(D("pv", lo, lo + n), D(P, b, b + n), D("th4", lo, lo + n), A.is_lt)
-            for P, b, lo, n in parts: vt(D("mk", lo, lo + n), D("pv", lo, lo + n), D("nk", lo, lo + n), A.mult)
+            for P, b, lo, n, o in parts: vt(D("nk", lo, lo + n), D(P, b, b + n), D("ci", lo, lo + n), A.add)
+            for P, b, lo, n, o in parts: vt(D("pv", lo, lo + n), D(P, b, b + n), D("th4", lo, lo + n), A.is_lt)
+            for P, b, lo, n, o in parts: vt(o or D("pv", lo, lo + n), D("pv", lo, lo + n), D("nk", lo, lo + n), A.mult)
 
-        def smin(q):
-            lo, hi = SC + 8 * s0[q], SC + 8 * s0[q + 1]
-            a, b = s0[q], s0[q + 1]
-            yield vt(D("ta", 4 * a, 4 * b), D("mk", lo, hi, 2), D("mk", lo + 1, hi, 2), A.min)
-            yield vt(D("tb", 2 * a, 2 * b), D("ta", 4 * a, 4 * b, 2), D("ta", 4 * a + 1, 4 * b, 2), A.min)
-            yield vt(D("bk", NV + a, NV + b), D("tb", 2 * a, 2 * b, 2), D("tb", 2 * a + 1, 2 * b, 2), A.min)
+        def smin(a, b): vscan(D("sm", 8 * a, 8 * b), D("s8", 8 * a, 8 * b), D("pv", SC + 8 * a, SC + 8 * b), 0.0, A.max, A.min)
 
-        def weave(*gs):
-            for _ in range(4):
-                for x in gs: next(x, None)
-        bv = D("bk", 0, NV)
-
-        def M(m, k=1): return D("mk", m * NV, (m + k) * NV)
-
-        def amin():
-            yield vt(D("tm0"), M(0, 2), M(2, 2), A.min)
-            yield vt(bv, D("tm0", 0, NV), D("tm0", NV, 2 * NV), A.min)
-
-        def bmin():
-            yield vt(D("tm0", 0, NV), M(4), M(5), A.min)
-            yield vt(D("tm1"), D("tm0", 0, NV), M(6), A.min)
-            yield vt(bv, bv, D("tm1"), A.min)
+        def vmin(c): vt(D("tm0"), D("tm0"), D("pv", 2 * c * NV, 2 * c * NV + 2 * NV), A.min)
         vgather(0)
         if t == 0: lists(list(range(2, 8)))
         sgather(0)
         vgather(1); vsums(0); sgather(1); ssums(0)
         vgather(2); vsums(1); sgather(2); vsums(2); sgather(3)
-        posts([("pd0", 0, 0, 4 * NV)]); weave(amin())
-        vgather(3); vsums(3); ssums(1)
-        vgather(4); vsums(4); ssums(2)
-        strides()
-        posts([("pd1", 0, 4 * NV, 3 * NV), ("pds", 0, SC, 8 * s0[2])]); weave(bmin(), smin(0), smin(1))
-        posts([("pu", 0, 7 * NV, NV), ("plf", 0, SC + 8 * s0[2], 8 * SGR[2])])
-        weave(smin(2), iter([vt(bv, bv, M(7), A.min)]))
-        vx(D("t1"), D("bk"))
+        vgather(3); vsums(3); ssums(1); ssums(2)
+        posts([("pd0", 0, 0, 4 * NV, D("mk")), ("pd1", 0, 4 * NV, 2 * NV, None)])
+        vt(D("tm0"), D("mk", 0, 2 * NV), D("mk", 2 * NV, 4 * NV), A.min)
+        strides(); vmin(2)
+        sa(D("dw"), D("c16"), F.Copy, 0.0, 0.0); steps()
+        posts([("pu", 0, 6 * NV, 2 * NV, None), ("pds", 0, SC, 8 * s0[2], None)]); vmin(3); smin(0, s0[2])
+        vt(D("bk", 0, NV), D("tm0", 0, NV), D("tm0", NV, 2 * NV), A.min)
+        if NV == 32: vx(D("t1", 0, 32), D("bk", 0, 32))
+        posts([("plf", 0, SC + 8 * s0[2], 8 * SGR[2], None)]); smin(s0[2], NS)
+        if NV == 32:
+            vx(D("t1", 32, 64), D("sm", 7, 8 * NS, 8))
+        else:
+            vc(D("bk", NV, 64), D("sm", 7, 8 * NS, 8)); vx(D("t1"), D("bk"))
         vscan(D("bsc"), D("s16"), D("t1"), 0.0, A.max, A.min)
         vc(D("bi"), D("bsc", 15, 64, 16)); vt(D("t0"), D("bsc", 15, 64, 16), D("i64"), A.add)
         vs(D("jb64"), D("bi"), 4032, A.bitwise_and)
-        vt(D("tt1"), D("t0"), D("jb64"), A.subtract); vs(D("jf"), D("jb64"), 64.0, A.add)
+        vs(D("jf"), D("jb64"), 64.0, A.add); vt(D("tt1"), D("t0"), D("jb64"), A.subtract)
         for b in range(2):
             for s in range(2):
                 c = 2 * b + s
@@ -375,68 +383,73 @@ def rank_program(g, core, T, topo):
         vt(D("cut"), D("oh"), D("got"), A.add)
         vx(D("r1"), D("z")); vc(D("l1"), D("plf", 0, 4))
         L1 = D("l1"); L4 = D("l4"); L16 = D("l16")
+
+        def places(k):
+            if k < nq: vt(D("pp", k, nk_, nq), D("pw", k, nk_, nq), D("sp"), A.add)
+            elif not last: vt(D("pp", nk_, np_), D("pw", nk_, np_), D("sp"), A.add)
         for x in range(2): sa(D("cl", x, 8, 2), D("cut"), F.Identity, 0.0, D("m%d" % x))
-        for c in range(4): sa(D("zc", 16 * c, 16 * c + 16), D("z64", 0, 16), F.Identity, D("cut", bs[c], bs[c] + 1))
+        pe(D("plf", 4, 8), [(D("u0"), D("cl", 0, 4)), (D("u1"), D("cl", 4, 8))])
         vc(D("r2"), IND(D("r1"), L1))
+        sa(D("lenb"), D("plf", 4, 8), F.Copy, 64.0, -1.0); sa(D("lenl"), D("plf", 4, 8), F.Copy, 64.0, -1.0)
+        pe(D("pu", 0, 1), [(D("blk"), D("lenb", q, q + 1)) for q in range(4)])
         vc(D("r3"), IND(D("r2"), L1))
         vt(D("rl"), IND(D("r3"), L1), D("mdg"), A.mult); sa(D("r4"), IND(D("r3"), L1), F.Copy)
+        sa(D("l64"), D("pu", 0, 1), F.Copy, 0.0, 0.015625); sa(D("l8k"), D("pu", 0, 1), F.Copy, 0.0, 8192.0); sa(D("lcol"), D("pu", 0, 1), F.Copy)
+        for c in range(4): sa(D("zc", 16 * c, 16 * c + 16), D("z64", 0, 16), F.Identity, D("cut", bs[c], bs[c] + 1))
         vscan(D("sl"), D("rst"), D("rl"), 0.0, A.mult, A.add)
-        pe(D("plf", 4, 8), [(D("u0"), D("cl", 0, 4)), (D("u1"), D("cl", 4, 8))])
-        vx(D("cr"), D("zc"))
         vc(L4, D("sl", 15, 64, 16))
-        sa(D("lenl"), D("plf", 4, 8), F.Copy, 64.0, -1.0)
-        for q in range(4): sa(D("lb%d" % q), D("blk"), F.Identity, 0.0, D("lenl", q, q + 1))
+        vs(D("sp"), D("kp"), D("l64"), A.mult, -0.4921875, A.add)
         vc(D("r8"), IND(D("r4"), L4))
-        vt(D("er"), D("cr"), D("ej"), A.add)
+        places(0)
         vc(D("r12"), IND(D("r8"), L4))
+        places(1)
         vt(D("rl2"), IND(D("r12"), L4), D("mdg"), A.mult); sa(D("r16"), IND(D("r12"), L4), F.Copy)
+        for q in range(4): sa(D("lb%d" % q), D("blk"), F.Identity, 0.0, D("lenl", q, q + 1))
+        places(2)
         vscan(D("sl2"), D("rst"), D("rl2"), 0.0, A.mult, A.add)
+        places(3)
         vc(L16, D("sl2", 15, 64, 16))
+        places(4)
+        sa(D("wa", 0, np_), D("pp", 0, np_), F.Relu, D("l8k"), -8192.0)
+        sa(D("pv", 0, np_), D("wa", 0, np_), F.Relu, D("lcol"), -1.0)
         vc(D("r32"), IND(D("r16"), L16))
+        vx(D("cr"), D("zc"))
         vc(D("r48"), IND(D("r32"), L16))
+        vt(D("er"), D("cr"), D("ej"), A.add)
         vt(D("rl3"), IND(D("r48"), L16), D("mdg"), A.mult)
-        vt(D("kr", 0, 64), IND(D("r48"), L16), D("jj"), A.add)
+        vt(D("kr"), IND(D("r48"), L16), D("jj"), A.add)
         vscan(D("sl3"), D("rst"), D("rl3"), 0.0, A.mult, A.add)
-        for q in range(4): vs(D("cc%d" % q, 0, 65), D("kr", 0, 65), D("sl3", 16 * q + 15, 16 * q + 16), A.subtract, D("qj", q, q + 1), A.is_gt)
-        pe(D("ppos", 0, 65), [(D("lb%d" % q), D("cc%d" % q, 0, 65)) for q in range(4)])
-        vs(D("ww"), D("kr", 0, 64), 262144.0, A.mult); vt(D("ew"), D("er"), D("ww"), A.add)
+        vs(D("ww"), D("kr"), 262144.0, A.mult)
+        for q in range(4): vs(D("cc%d" % q), D("kr"), D("sl3", 16 * q + 15, 16 * q + 16), A.subtract, D("qj", q, q + 1), A.is_gt)
+        pe(D("ppos", 0, 64), [(D("lb%d" % q), D("cc%d" % q)) for q in range(4)])
+        vt(D("pq", 0, np_), D("pp", 0, np_), D("pv", 0, np_), A.subtract)
         vt(D("pm"), D("ppos", 0, 64), D("mdg"), A.mult)
         vc(D("pi"), D("ppos", 0, 64))
         vscan(D("ps"), D("rst"), D("pm"), 0.0, A.mult, A.add)
-        sa(D("lcol"), D("ppos", 64, 65), F.Copy)
         vs(D("pr"), D("pi"), 15, A.bitwise_and)
+        vt(D("ew"), D("er"), D("ww"), A.add)
         vs(D("tl4"), D("ps", 15, 64, 16), 0.0625, A.mult, -0.46875, A.add)
         vt(D("vvv"), D("ew"), D("pr"), A.subtract); vs(D("mlt"), D("pr"), D("rcol"), A.is_le)
         vc(D("tl", 0, 4), D("tl4")); vs(D("tl", 4, 8), D("tl4"), 1.0, A.add)
-        vt(D("vv", 0, 64), D("vvv"), D("mlt"), A.mult); vs(D("vv", 64, 128), D("vvv"), 16.0, A.add)
-        vs(D("si"), D("kp"), D("lcol"), A.mult)
+        vt(D("vv", 0, 64), D("vvv"), D("mlt"), A.mult); sa(D("vv", 64, 128), D("vvv"), F.Copy, 16.0)
+        if not last: vt(D("lm"), D("pq", nk_, np_), D("mdg"), A.mult)
         vc(IND(D("dw"), D("tl")), D("vv"))
-        vs(D("sp"), D("si"), 6, A.logical_shift_right)
+        if not last: vscan(D("lsc"), D("rst"), D("lm"), 0.0, A.mult, A.add)
         vscan(D("ls", 0, LAY0), D("c16", 0, LAY0), D("dw", 0, LAY0), -1000.0, A.add, A.max)
+        if not last: vc(D("lx"), D("lsc", 15, 64, 16))
         vc(D("lsi", 0, LAY0), D("ls", 0, LAY0))
         vscan(D("ls", LAY0, 256), D("c16", LAY0, 256), D("dw", LAY0, 256), D("ls", LAY0 - 1, LAY0), A.add, A.max)
         vs(D("lsa", 0, LAY0), D("lsi", 0, LAY0), 4095, A.bitwise_and)
         vc(D("lsi", LAY0, 256), D("ls", LAY0, 256))
         vc(D("lay", 0, LAY0), D("lsa", 0, LAY0))
         vs(D("lsa", LAY0, 256), D("lsi", LAY0, 256), 4095, A.bitwise_and)
+        vc(D("kl", 0, nk_), D("pq", 0, nk_))
         vc(D("lay", LAY0, 256), D("lsa", LAY0, 256))
         sa(D("xp", 0, 16 * LAY0), IND(D(X), D("lay", 0, LAY0)), F.Copy)
         sa(D("xp", 16 * LAY0, 16 * LAYS[t]), IND(D(X), D("lay", LAY0, LAYS[t])), F.Copy)
-        if not last: vt(D("lp"), D("h63"), D("sp"), A.add)
-        for k in range(nq): vt(D("pp", k, 64 * nq, nq), D("pw", k, 64 * nq, nq), D("sp"), A.add)
-        if not last:
-            vs(D("lw"), D("lp"), D("lcol"), A.is_ge, D("lcol"), A.mult)
-        vs(D("pv", 0, 64 * nq), D("pp", 0, 64 * nq), D("lcol"), A.is_ge, D("lcol"), A.mult)
-        if not last: vt(D("lq"), D("lp"), D("lw"), A.subtract)
-        vt(D("pq", 0, 64 * nq), D("pp", 0, 64 * nq), D("pv", 0, 64 * nq), A.subtract)
-        if not last: vt(D("lm"), D("lq"), D("mdg"), A.mult)
-        vc(D("kl", 0, 64 * nq), D("pq", 0, 64 * nq))
-        if not last: vscan(D("lsc"), D("rst"), D("lm"), 0.0, A.mult, A.add)
         vc(D("xp", 16 * LAYS[t], 4096), IND(D(X), D("lay", LAYS[t], 256)))
-        if not last: vc(D("lx"), D("lsc", 15, 64, 16))
-        w = width(t)
-        XN = "yb" if last else ("xa" if t == 1 else "xb")
-        KB = "kb%d" % t
+        w = WIDTH[t]
+        n = w // 32
         if not last:
             XK = "xk%d" % t; XLN = "xl%d" % (t + 1)
             vc(D(XK), IND(D("xp"), D("lx")))
@@ -446,55 +459,25 @@ def rank_program(g, core, T, topo):
                 d = T.cores[(rank + k + 1) % n_ranks]
                 rid, pid = topo.addr(d, core)
                 en = topo.engines(core, d)
-                mask = (1 << en[2 * k]) + (1 << en[2 * k + 1])
-                trs.append(RemoteDMATransfer(dst_ids=[DstId(rid=rid, pnc=pid)], dma_engine_mask=mask, remote_sem=T.sem["xs%d" % (t + 1)],
+                trs.append(RemoteDMATransfer(dst_ids=[DstId(rid=rid, pnc=pid)], dma_engine_mask=(1 << en[2 * k]) + (1 << en[2 * k + 1]), remote_sem=T.sem["xs%d" % (t + 1)],
                                              src=T[XK][:, 16 * k:16 * k + 16], dst=T[XLN][:, 16 * rank:16 * rank + 16]))
-            g.remote_dma_fused(trs, local_sem=T.sem["ux%d" % t])
-            for k in range(1, 4):
-                p = (rank - k) % n_ranks
-                source("XS%d" % (t + 1), "xs%d" % (t + 1), 6, D(XLN, 16 * p, 16 * p + 16)[1])
+            g.remote_dma_fused(trs, local_sem=T.sem.tx)
+            sent[0] += 6
+            source("XS%d" % (t + 1), "xs%d" % (t + 1), 6, [(XLN, 16 * p, 16 * p + 16, 1) for p in range(n_ranks) if p != rank])
         for k in range(4):
-            n = w // 32
-            if k < 3: oa = D(KB, k * w, k * w + w // 2); ob = D(KB, k * w + w // 2, k * w + w)
-            else: oa = D(XN, rank * w, rank * w + w // 2); ob = D(XN, rank * w + w // 2, rank * w + w)
-            if k == 3 and not last: sa(oa, IND(D("xp"), D("kl", 2 * k * n, 2 * k * n + n)), F.Copy)
-            else: vc(oa, IND(D("xp"), D("kl", 2 * k * n, 2 * k * n + n)))
-            sa(ob, IND(D("xp"), D("kl", 2 * k * n + n, 2 * k * n + 2 * n)), F.Copy)
-            if k < 3:
-                d = T.cores[(rank + k + 1) % n_ranks]
-                rid, pid = topo.addr(d, core)
-                sync_for("g", [], D(KB, k * w, k * w + w)[1])
-                ar = T.sem["ar%d_%d" % (t, k + 1)]; tx = T.sem["tx%d" % t]
-                mask = topo.mask(core, d)
-                f = RELAY[t][k]
-                m = k * w + w - f
-                if f:
-                    hc = helpers(core)[k]
-                    hrid, hpid = topo.addr(hc, core)
-                    he = hop_engines(core, hc, d)
-                    hop = RemoteDMATransfer(dst_ids=[DstId(rid=hrid, pnc=hpid)], dma_engine_mask=sum(1 << e for e in he), remote_sem=T.sem["ra%d" % t], src=T[KB][:, m:k * w + w], dst=T[KB][:, m:k * w + w])
-                    on = RemoteDMATransfer(dst_ids=[DstId(rid=rid, pnc=pid)], dma_engine_mask=mask, remote_sem=ar, src=T[KB][:, k * w:m], dst=T[XN][:, rank * w:rank * w + w - f])
-                    for trs in ([[hop, on]] if 2 * f == w else [[hop], [on]]): g.remote_dma_fused(trs, local_sem=tx)
-                    sent[t] += len(he)
-                else:
-                    g.remote_dma(T[XN][:, rank * w:rank * w + w], T[KB][:, k * w:k * w + w], ar, tx, pid, rid, mask)
-                sent[t] += len(topo.engines(core, d))
+            buf, o = (SRC[t], k * w) if k < 3 else (DST[t], rank * w)
+            vc(D(buf, o, o + w // 2), IND(D("xp"), D("kl", 2 * k * n, 2 * k * n + n)))
+            sa(D(buf, o + w // 2, o + w), IND(D("xp"), D("kl", 2 * k * n + n, 2 * k * n + 2 * n)), F.Copy)
+            if k < 3: send(t, k)
         if not last:
             vc(D(XLN, 16 * rank, 16 * rank + 16), D(XK, 48, 64))
-            vm(D("dw"), 0.0)
-        for k in range(1, 4):
-            p = (rank - k) % n_ranks
-            cnt = len(topo.engines(T.cores[p], core))
-            if RELAY[t][k - 1]: cnt += len(topo.engines(helpers(T.cores[p])[k - 1], core))
-            source("AR%d_%d" % (t, k), "ar%d_%d" % (t, k), cnt, D(XN, p * w, p * w + w)[1])
+            for k in range(3): arrival(t, k)
 
     for k in range(4):
-        p = (rank - k) % n_ranks
+        p = rank if k == 0 else arrival(2, k - 1)
         sync_for("y", [], D("yb", p * 512, p * 512 + 512)[1])
         g.sync.dma_start(T.y[:, p * 512:p * 512 + 512], T.yb[:, p * 512:p * 512 + 512]).then_inc(T.sem.stor, 16)
     g.sync.wait_ge(T.sem.stor, 64)
-    for t in range(3):
-        g.wait_ge(T.sem["tx%d" % t], sent[t])
-        if t < 2: g.wait_ge(T.sem["ux%d" % t], 6)
+    g.wait_ge(T.sem.tx, sent[0])
     for q in ("v", "s", "t", "g"):
         wait("g", q, count[q])

@@ -3,34 +3,38 @@ from concourse.mybir import dt, AluOpType as A, AxisListType, ActivationFunction
 
 NV = 32
 NS = 64 - NV
-SCH = [8, 6, 6, NS - 20]
-SGR = [12, 12, NS - 24]
-ABS = (0, 1)
+SCH = ([16, 4, 4, 8], [8, 6, 10, 8])
+SGR = [12, 12, 8]
+ABSR = ((0, 1), (0,))
+ORDER = "g0 g1 g2 c0 g3 p0 g4 r1 c1 p1 q0 g5 v0 g6 r2 p2 v0 v1 c2 q1 g7 v1 s0 r3 p3 c3 q2 v1 s0 v2 s0 v2 s1 v2 s1 v3 s1 s2 v3 s2 v3 s2"
 WIDTH = (1024, 1024, 512)
-RELAY = ((512, 512, 128), (512, 512, 128), (256, 256, 0))
-LAYS = (144, 144, 144)
+_MID = ((0, 256, 256, 0), (0, 256, 256, 1), (1, 512, 512, 2), (2, 896, 128, 3))
+PLAN = (_MID, _MID, ((0, 256, 256, 0), (1, 256, 256, 1), (2, 512, 0, 0)))
+LAYS = (138, 138, 138)
 LAY0 = 64
+OWNV = 6
 BIG = 16777216
+ROUND = 12582912
 SC = NV * 8
 
 _F32 = [("wtf", 1), ("kmf", 24), ("thf", 8), ("mdg", 64), ("rst", 64), ("rcol", 1), ("qcol", 4), ("qj", 4), ("iq", 4), ("i64", 4), ("ib", 4), ("idf", 4), ("df", 4), ("defn", 4),
         ("s16", 64), ("s32", 128), ("s8", 8 * NS), ("j64", 64), ("jp", 64), ("jm0", 64), ("jm1", 64), ("ej", 64), ("jj", 64), ("z64", 64), ("m0", 1), ("m1", 1), ("mm0", 4), ("mm1", 4),
-        ("c16", 256), ("kp", 64), ("th4", 512),
-        ("nx", 64), ("uf", 64), ("uk", 512), ("nk", 512), ("mk", 4 * NV), ("tm0", 2 * NV), ("sm", 8 * NS),
+        ("kp", 64), ("th4", 512),
+        ("nx", 64), ("uf", 64), ("uk", 512), ("nk", 512), ("tm0", 2 * NV), ("sm", 8 * NS),
         ("bk", 64), ("t1", 64), ("bsc", 64), ("t0", 4), ("jf", 4), ("tt1", 4),
-        ("pm0", 128), ("px", 128), ("t2", 128), ("acs", 128), ("got", 4), ("cut", 4), ("pf", 4), ("z", 64), ("zc", 64), ("r1", 64), ("cr", 64), ("er", 64),
+        ("pm0", 128), ("px", 128), ("t2", 128), ("acs", 128), ("got", 4), ("cut", 4), ("z", 64), ("zc", 64), ("r1", 64), ("cr", 64), ("md16", 64),
         ("r2", 64), ("r3", 64), ("r4", 64), ("rl", 64), ("sl", 64), ("r8", 64), ("r12", 64), ("r16", 64), ("rl2", 64), ("sl2", 64), ("r32", 64), ("r48", 64),
-        ("kr", 64), ("rl3", 64), ("sl3", 64), ("lenl", 4), ("pm", 64), ("ps", 64), ("mlt", 64), ("ww", 64), ("ew", 64), ("vvv", 64), ("vv", 128),
-        ("dw", 256), ("ls", 256), ("hf", 64), ("hp", 64), ("lcol", 1), ("l64", 1), ("l8k", 1), ("pp", 320), ("wa", 320), ("pq", 320), ("lm", 64), ("lsc", 64)]
-_I32 = [("wti", 1), ("kmi", 24), ("thi", 8), ("ia", 64), ("ibb", 64), ("icc", 1), ("id4", 4), ("ixo", NV), ("iu", 128), ("ui", 64), ("um", 64), ("uu", 64), ("vi", 64),
-        ("cp", 512), ("ci", 512), ("bi", 4), ("jb64", 4), ("ai", 4), ("pa", 4), ("oh", 4), ("pi", 64), ("pr", 64), ("tl4", 4), ("lsi", 256), ("lsa", 256),
+        ("kr", 64), ("rl3", 64), ("sl3", 64), ("lenl", 4), ("pm", 64), ("ps", 64), ("mlt", 128), ("vv", 128),
+        ("r32c", 1), ("cf", 512), ("idn", 128), ("one", 128), ("dk", 256), ("dw", 256), ("ls", 256), ("hf", 64), ("hp", 64), ("lcol", 1), ("l64", 1), ("l8k", 1), ("pp", 320), ("wa", 320), ("pq", 320), ("lm", 64), ("lsc", 64)]
+_I32 = [("wti", 1), ("kmi", 24), ("thi", 8), ("icc", 1), ("id4", 4), ("ixo", NV + 4), ("iu", 128), ("ui", 64), ("um", 64), ("uu", 64), ("vi", 64),
+        ("cp", 512), ("ci", 512), ("bi", 4), ("jb64", 4), ("ai", 4), ("pa", 4), ("oh", 4), ("pi", 64), ("pr", 64), ("lsi", 128),
         ("h31", 64), ("sp", 64)]
 _BF = [("xa", 4096), ("xb", 4096), ("xl0", 64), ("xl1", 64), ("xl2", 64), ("xp", 4096), ("kb0", 3072), ("kb1", 3072), ("kb2", 1536), ("yb", 2048),
-       ("xk0", 64), ("xk1", 64), ("ones", 128), ("bt", 128), ("blk", 128), ("wb", 128), ("sel", 144), ("sel2", 144), ("seln", 144), ("nb", 128),
+       ("xk0", 64), ("xk1", 64), ("ones", 128), ("bt", 128), ("blk", 128), ("wb", 128), ("sel", 144), ("sel2", 144), ("seln", 144), ("nb", 128), ("n75", 128),
        ("u0", 128), ("u1", 128), ("b32", 128), ("b3t", 128), ("wm", 128), ("wm2", 128), ("lb0", 128), ("lb1", 128), ("lb2", 128), ("lb3", 128),
        ("xr", 16 * NV), ("dv", 128 * NV), ("av", 128 * NV), ("as", 128 * NS),
        ("pl", 8), ("cl", 8), ("lenb", 4), ("cc0", 64), ("cc1", 64), ("cc2", 64), ("cc3", 64)]
-_U16 = [("xo", NV), ("of", 512), ("l1", 4), ("l4", 4), ("l16", 4), ("tl", 8), ("lay", 256), ("kl", 256), ("lx", 4)]
+_U16 = [("xo", NV), ("of", 512), ("l1", 4), ("l4", 4), ("l16", 4), ("tl", 8), ("lay", 256), ("kl", 256), ("lx", 4), ("zl", 4)]
 _PS = ["pu", "pd0", "pd1", "pds", "pv", "plf", "ppos", "pw"]
 _OWN = ("xa", "xb", "xl0", "xl1", "xl2", "kb0", "kb1", "kb2", "yb", "xk0", "xk1", "wti", "kmi", "thi")
 SCRATCH = {}
@@ -45,8 +49,8 @@ for _l, _d, _b, _al in ((_F32, "float32", "ff", 8), (_I32, "int32", "ii", 8), (_
     SCRATCH[_b] = ("sbuf", [128, _at], _d)
 for _n in _PS:
     SCRATCH[_n] = ("psum", [128, 512], "float32"); PLACE[_n] = (_n, 0, 512)
-SEMAPHORES = ["sv", "ss", "st", "sg", "lw", "lk", "lt", "lx0", "lx1", "xs1", "xs2", "stor", "tx", "ra0", "ra1", "ra2"]
-SEMAPHORES += ["ar%d_%d" % (t, k) for t in range(3) for k in range(3)]
+SEMAPHORES = ["sv", "ss", "st", "sg", "lw", "lk", "lt", "lx0", "lx1", "xs1", "xs2", "stor", "tx"]
+SEMAPHORES += ["ar%d_%d" % (t, k) for t in range(3) for k in range(3)] + ["ra%d_%d" % (t, i) for t in range(3) for i in range(len(PLAN[t]))]
 
 
 def rank_program(g, core, T, topo):
@@ -59,22 +63,28 @@ def rank_program(g, core, T, topo):
     def hop_engines(rc, hc, d):
         off = topo.engines(rc, d)
         return [e for e in topo.engines(rc, hc) if e not in off]
+
+    def pieces(t):
+        at = [0, 0, 0]
+        for i, (k, on, by, h) in enumerate(PLAN[t]):
+            yield i, k, at[k], on, by, h
+            at[k] += on + by
     rank = T.rank_of(core)
     if rank is None:
         for r, rc in enumerate(T.cores):
             hs = helpers(rc)
             if core not in hs: continue
-            k = hs.index(core)
             n = 0
             for t in range(3):
-                if k >= len(RELAY[t]) or not RELAY[t][k]: continue
-                d = T.cores[(r + k + 1) % n_ranks]
-                rid, pid = topo.addr(d, core)
-                w = WIDTH[t]; f = RELAY[t][k]
-                g.wait_ge(T.sem["ra%d" % t], len(hop_engines(rc, core, d)))
-                g.remote_dma(T[DST[t]][:, r * w + w - f:r * w + w], T[SRC[t]][:, k * w + w - f:k * w + w], T.sem["ar%d_%d" % (t, k)], T.sem.tx, pid, rid, topo.mask(core, d))
-                n += len(topo.engines(core, d))
-                g.wait_ge(T.sem.tx, n)
+                for i, k, lo, on, by, h in pieces(t):
+                    if not by or hs[h] != core: continue
+                    d = T.cores[(r + k + 1) % n_ranks]
+                    rid, pid = topo.addr(d, core)
+                    w = WIDTH[t]; a = lo + on
+                    g.wait_ge(T.sem["ra%d_%d" % (t, i)], len(hop_engines(rc, core, d)))
+                    g.remote_dma(T[DST[t]][:, r * w + a:r * w + a + by], T[SRC[t]][:, k * w + a:k * w + a + by], T.sem["ar%d_%d" % (t, k)], T.sem.tx, pid, rid, topo.mask(core, d))
+                    n += len(topo.engines(core, d))
+            if n: g.wait_ge(T.sem.tx, n)
         return
     queue = {"v": g.vector, "s": g.scalar, "t": g.tensor, "g": g, "y": g.sync}
     semname = {"v": "sv", "s": "ss", "t": "st", "g": "sg"}
@@ -161,15 +171,15 @@ def rank_program(g, core, T, topo):
         c1, k1 = col(bias); c2, k2 = col(scale)
         run("s", o, a[1] + k1 + k2, lambda: g.scalar.activation(o[0], a[0], f, bias=c1, scale=c2))
 
-    def pe(o, *parts):
+    def pe(o, *parts, start=True, stop=True):
         i = []
         r = None
         for p, pairs in enumerate(parts):
             j = [k for a, b in pairs for k in a[1] + b[1]]
-            sync_for("t", o[1] if p == 0 else [], j)
+            sync_for("t", o[1] if p == 0 and start else [], j)
             i = i + j
             for n, (a, b) in enumerate(pairs):
-                r = g.tensor.matmul(o[0], a[0], b[0], p == 0 and n == 0, p == len(parts) - 1 and n == len(pairs) - 1)
+                r = g.tensor.matmul(o[0], a[0], b[0], start and p == 0 and n == 0, stop and p == len(parts) - 1 and n == len(pairs) - 1)
         note("t", done("t", r), o[1], i)
 
     def gi(o, pattern, base, cm):
@@ -182,74 +192,84 @@ def rank_program(g, core, T, topo):
         queue[q].dma_start(o[0], src).then_inc(T.sem[sem], 16)
         source(sem, sem, 16, o[1])
 
-    def send(t, k):
+    def send(t, i, k, lo, on, by, h):
         d = T.cores[(rank + k + 1) % n_ranks]
         rid, pid = topo.addr(d, core)
-        w = WIDTH[t]; f = RELAY[t][k]; m = k * w + w - f; at = rank * w
-        S = T[SRC[t]]; ar = T.sem["ar%d_%d" % (t, k)]
-        sync_for("g", [], D(SRC[t], k * w, k * w + w)[1])
-        on = RemoteDMATransfer(dst_ids=[DstId(rid=rid, pnc=pid)], dma_engine_mask=topo.mask(core, d), remote_sem=ar, src=S[:, k * w:m], dst=T[DST[t]][:, at:at + w - f])
-        calls = [[on]]
-        if f:
-            hc = helpers(core)[k]
+        w = WIDTH[t]; a = k * w + lo; m = a + on
+        S = T[SRC[t]]
+        sync_for("g", [], D(SRC[t], a, m + by)[1])
+        trs = []
+        if by:
+            hc = helpers(core)[h]
             hrid, hpid = topo.addr(hc, core)
             he = hop_engines(core, hc, d)
-            hop = RemoteDMATransfer(dst_ids=[DstId(rid=hrid, pnc=hpid)], dma_engine_mask=sum(1 << e for e in he), remote_sem=T.sem["ra%d" % t], src=S[:, m:k * w + w], dst=S[:, m:k * w + w])
-            calls = [[hop, on]] if 2 * f == w else [[hop], [on]]
+            trs.append(RemoteDMATransfer(dst_ids=[DstId(rid=hrid, pnc=hpid)], dma_engine_mask=sum(1 << e for e in he), remote_sem=T.sem["ra%d_%d" % (t, i)], src=S[:, m:m + by], dst=S[:, m:m + by]))
             sent[0] += len(he)
-        for trs in calls: g.remote_dma_fused(trs, local_sem=T.sem.tx)
-        sent[0] += len(topo.engines(core, d))
+        if on:
+            trs.append(RemoteDMATransfer(dst_ids=[DstId(rid=rid, pnc=pid)], dma_engine_mask=topo.mask(core, d), remote_sem=T.sem["ar%d_%d" % (t, k)], src=S[:, a:m], dst=T[DST[t]][:, rank * w + lo:rank * w + lo + on]))
+            sent[0] += len(topo.engines(core, d))
+        for call in ([trs] if on == by else [[x] for x in trs]): g.remote_dma_fused(call, local_sem=T.sem.tx)
 
     def arrival(t, k):
         p = (rank - k - 1) % n_ranks
-        cnt = len(topo.engines(T.cores[p], core))
-        if RELAY[t][k]: cnt += len(topo.engines(helpers(T.cores[p])[k], core))
+        cnt = sum((len(topo.engines(T.cores[p], core)) if on else 0) + (len(topo.engines(helpers(T.cores[p])[h], core)) if by else 0) for i, k2, lo, on, by, h in pieces(t) if k2 == k)
         source("AR%d_%d" % (t, k), "ar%d_%d" % (t, k), cnt, D(DST[t], p * WIDTH[t], (p + 1) * WIDTH[t])[1])
         return p
 
-    load("y", "lx0", D("xa", 0, 2048), T.gen0[:, 0:2048])
-    load("s", "lw", D("wti"), T.wt[:]); load("s", "lk", D("kmi"), T.km[:])
-    load("y", "lx1", D("xa", 2048, 4096), T.gen0[:, 2048:4096])
-    load("s", "lt", D("thi"), T.th[:])
+    def own(t):
+        yield None
+        for a in range(0, 4 * OWNV, OWNV):
+            yield vc(D(DST[t], rank * 1024 + 16 * a, rank * 1024 + 16 * (a + OWNV)), IND(D("xp"), D("kl", 192 + a, 192 + a + OWNV)))
+
+    def rest(t):
+        sa(D(DST[t], rank * 1024 + 64 * OWNV, rank * 1024 + 1024), IND(D("xp"), D("kl", 192 + 4 * OWNV, 256)), F.Copy)
+        for k in range(3): arrival(t, k)
+
+    def weave(*gs):
+        for _ in range(6):
+            for x in gs: next(x, None)
+
+    load("y", "lx0", D("xa", 64 * NV, 4096), T.gen0[:, 64 * NV:4096])
+    load("s", "lw", D("wti"), T.wt[:]); load("s", "lt", D("thi"), T.th[:])
+    load("y", "lx1", D("xa", 0, 64 * NV), T.gen0[:, 0:64 * NV])
+    load("s", "lk", D("kmi"), T.km[:])
 
     vm(D("ones"), 1.0); vm(D("sel"), 0.0)
-    gi(D("z64"), [[0, 64]], 0, 0)
+    gi(D("icc"), [[0, 1]], 0, 1); gi(D("iu"), [[1, 128]], 128, -1)
     gsel(D("bt"), D("ones"), [[-16, 8], [0, 16]], A.is_ge, 0, 1)
-    gsel(D("blk"), D("bt"), [[16, 8], [0, 16]], A.is_ge, 15, -1)
-    gi(D("icc"), [[0, 1]], 0, 1); gi(D("ibb"), [[1, 64]], 0, 0); gi(D("ia"), [[1, 64]], 128, -1)
-    gi(D("ixo"), [[1, NV]], 0, 0)
-    gi(D("j64"), [[64, 64]], 0, 0); gi(D("iq"), [[16, 4]], 0, 0)
-    gi(D("id4"), [[0, 4]], 0, 64); gi(D("ib"), [[2048, 2], [0, 2]], 0, 0); gi(D("idf"), [[0, 2], [2048, 2]], 0, 0)
-    gi(D("iu"), [[1, 128]], 128, -1)
     gsel(D("b3t"), D("ones"), [[-32, 4], [0, 32]], A.is_ge, 0, 1)
+    gsel(D("blk"), D("bt"), [[16, 8], [0, 16]], A.is_ge, 15, -1)
     gsel(D("b32"), D("b3t"), [[32, 4], [0, 32]], A.is_ge, 31, -1)
-    gi(D("nb"), [[0, 128]], -131072, 0)
-    vm(D("s32"), float(-2 * BIG)); vm(D("s8"), float(-2 * BIG)); vm(D("s32", 0, 128, 32), 1.0); vm(D("s8", 0, 8 * NS, 8), 1.0)
-    vs(D("sel", 15, 143, 16), D("blk", 0, 128, 16), 4096.0, A.mult)
+    gi(D("id4"), [[0, 4]], 0, 64); gi(D("ib"), [[2048, 2], [0, 2]], 0, 0); gi(D("idf"), [[0, 2], [2048, 2]], 0, 0)
+    gi(D("ixo", 0, NV), [[1, NV]], 0, 0); gi(D("ixo", NV, NV + 4), [[1, 2], [2, 2]], 0, 0)
+    gi(D("j64"), [[64, 64]], 0, 0); gi(D("iq"), [[16, 4]], 0, 0)
+    vm(D("z64"), 0.0); vm(D("nb"), -131072.0); vm(D("n75"), -7.5 / 128); vm(D("one"), 1.0); vm(D("mlt", 64, 128), 1.0); vm(D("rst"), 1.0)
+    vm(D("s32"), float(-2 * BIG)); vm(D("s8"), float(-2 * BIG)); vm(D("s16"), float(-2 * BIG))
+    vm(D("s32", 0, 128, 32), 1.0); vm(D("s8", 0, 8 * NS, 8), 1.0); vm(D("s16", 0, 64, 16), 1.0); vm(D("rst", 0, 64, 16), 0.0)
     vs(D("pi", 0, 1), D("icc"), 15, A.bitwise_and); vs(D("pr", 0, 1), D("icc"), 4, A.logical_shift_right, 1, A.bitwise_and)
+    vs(D("lsi"), D("iu"), 15, A.bitwise_and)
     vc(D("rcol"), D("pi", 0, 1)); vc(D("m1"), D("pr", 0, 1))
-    vs(D("um"), D("ibb"), 15, A.bitwise_and); vs(D("ui"), D("ia"), 15, A.bitwise_and)
-    vs(D("rst"), D("um"), 0.0, A.not_equal); vs(D("mdg"), D("ui"), 0.0, A.is_equal)
-    vc(D("xo"), D("ixo"))
-    vc(D("wtf"), D("wti")); vc(D("kmf"), D("kmi"))
+    vs(D("wm"), D("lsi"), 0.0, A.is_equal); vs(D("mdg"), D("lsi", 0, 64), 0.0, A.is_equal); vs(D("md16"), D("lsi", 0, 64), 0.0, A.is_equal, 0.0625, A.mult)
+    vs(D("sel", 15, 143, 16), D("blk", 0, 128, 16), 4096.0, A.mult)
+    vc(D("wtf"), D("wti"))
+    vt(D("wm2"), D("wm"), D("b32"), A.mult)
     vs(D("wb"), D("blk"), D("wtf"), A.mult)
-    vs(D("bi"), D("id4"), 2047, A.bitwise_and); vs(D("ci", 0, 128), D("iu"), 15, A.bitwise_and)
-    vt(D("i64"), D("bi"), D("ib"), A.add); vt(D("df"), D("bi"), D("idf"), A.add); vs(D("wm"), D("ci", 0, 128), 0.0, A.is_equal)
+    vs(D("bi"), D("id4"), 2047, A.bitwise_and)
+    vc(D("xo"), D("ixo", 0, NV)); vc(D("zl"), D("ixo", NV, NV + 4))
+    vt(D("i64"), D("bi"), D("ib"), A.add); vt(D("df"), D("bi"), D("idf"), A.add)
     vs(D("defn"), D("df"), -4096.0, A.add)
     vs(D("thf"), D("thi"), 4096.0, A.mult, float(-BIG), A.add)
-    vt(D("wm2"), D("wm"), D("b32"), A.mult)
+    sa(D("m0"), D("m1"), F.Copy, 1.0, -1.0); sa(D("r32c"), D("rcol"), F.Copy, 32.0)
     sa(D("sel2"), D("sel"), F.Copy, 0.0, 2.0); sa(D("seln"), D("sel"), F.Copy, 0.0, -1.0)
-    sa(D("m0"), D("m1"), F.Copy, 1.0, -1.0)
     sa(D("mm1"), D("z64", 0, 4), F.Identity, D("m1")); sa(D("mm0"), D("z64", 0, 4), F.Identity, D("m0"))
-    sa(D("s16"), D("rst"), F.Copy, 1.0, float(-2 * BIG))
-    sa(D("jj"), D("j64"), F.Copy, 0.0, 1.0 / 4096); sa(D("ej"), D("j64"), F.Identity, D("rcol"))
+    sa(D("jj"), D("j64"), F.Copy, 0.0, 1.0 / 4096); sa(D("ej"), D("j64"), F.Identity, D("r32c"))
     sa(D("qcol"), D("iq"), F.Identity, D("rcol")); sa(D("qj"), D("qcol"), F.Copy, 0.0, 0.015625)
     for m in range(8):
         sa(D("th4", m * NV, m * NV + NV), D("z64", 0, NV), F.Identity, D("thf", m, m + 1))
         sa(D("th4", SC + m, 512, 8), D("z64", 0, NS), F.Identity, D("thf", m, m + 1))
+    gsel(D("idn"), D("one"), [[-1, 128]], A.is_equal, 0, 1)
     gsel(D("u0"), D("wm2"), [[0, 4], [1, 2], [0, 16]], A.is_equal, 0, 0)
     gsel(D("u1"), D("wm2"), [[0, 4], [1, 2], [0, 16]], A.is_gt, 0, 0)
-    gi(D("c16"), [[0, 256]], 16, 0)
     gi(D("kp", 0, 48), [[1, 3], [4, 16]], 1, 0); gi(D("kp", 48, 64), [[4, 16]], 0, 0)
     gi(D("jp"), [[64, 64]], 64, 0)
     for b in range(2):
@@ -264,57 +284,61 @@ def rank_program(g, core, T, topo):
 
         def times(o, lo, hi, m):
             k = D("kmf", t * 8 + m, t * 8 + m + 1)
-            if t or (lo == 0 and m > 1): sa(o, D("uf", lo, hi), F.Identity, 0.0, k)
-            else: vs(o, D("um", lo, hi), k, A.mult)
+            if lo == 0 and t == 0: vs(o, D("um", lo, hi), k, A.mult)
+            else: sa(o, D("uf", lo, hi), F.Identity, 0.0, k)
 
-        def offsets(lo, hi):
-            vs(D("ci", lo, hi), D("cp", lo, hi), 4095, A.bitwise_and); vc(D("of", lo, hi), D("ci", lo, hi))
+        def row(n, e, m):
+            return D(n, SC + m, 512, 8) if e else D(n, m * NV, m * NV + NV)
 
-        def lists(ms):
-            for m in ms: times(D("uk", m * NV, m * NV + NV), 0, NV, m)
-            for m in ms: vt(D("cp", m * NV, m * NV + NV), D("uk", m * NV, m * NV + NV), D("vi", 0, NV), A.add)
-            offsets(ms[0] * NV, ms[-1] * NV + NV)
+        def products(e):
+            if e: sa(D("nx", NV, 64), D(XL, NV, 64), F.Copy, 0.0, -1.0)
+            for m in range(8): times(row("uk", e, m), NV * e, 64 if e else NV, m)
 
-        def slists():
-            sa(D("nx", NV, 64), D(XL, NV, 64), F.Copy, 0.0, -1.0)
-            for m in range(8): times(D("uk", SC + m, 512, 8), NV, 64, m)
-            for m in range(8): vt(D("cp", SC + m, 512, 8), D("uk", SC + m, 512, 8), D("vi", NV, 64), A.add)
-            offsets(SC, 512)
-        if t == 0: vc(D(XL), D(X, 63, 4096, 64))
-        sa(D("xr"), IND(D(XL), D("xo")), F.Copy)
-        pe(D("pu", 0, 64), [(D("wb"), D(XL))])
-        vc(D("ui"), D("pu", 0, 64)); vs(D("um"), D("ui"), 4095, A.bitwise_and)
-        if t: vc(D("uf"), D("um"))
-        vt(D("uu"), D("um"), D("um"), A.mult); vs(D("vi"), D("uu"), 5, A.logical_shift_right)
+        def lists(e, m0=0, m1=8):
+            lo, hi = (SC, 512) if e else (m0 * NV, m1 * NV)
+            yield [vt(row("cp", e, m), row("uk", e, m), D("vi", NV * e, 64 if e else NV), A.add) for m in range(m0, m1)]
+            yield vs(D("ci", lo, hi), D("cp", lo, hi), 4095, A.bitwise_and)
+            yield vc(D("of", lo, hi), D("ci", lo, hi))
+            yield vc(D("cf", lo, hi), D("ci", lo, hi))
+        def hashes(lo, hi):
+            if t == 0: vc(D(XL, lo, hi), D(X, 64 * lo + 63, 64 * hi, 64))
+            yield pe(D("pu", lo, hi), [(D("wb"), D(XL, lo, hi))])
+            yield vc(D("ui", lo, hi), D("pu", lo, hi))
+            yield vs(D("um", lo, hi), D("ui", lo, hi), 4095, A.bitwise_and)
+            if t or lo: vc(D("uf", lo, hi), D("um", lo, hi))
+            yield vt(D("uu", lo, hi), D("um", lo, hi), D("um", lo, hi), A.mult)
+            yield vs(D("vi", lo, hi), D("uu", lo, hi), 5, A.logical_shift_right)
         if t == 0:
-            lists([0, 1]); vc(D("uf"), D("um")); slists()
+            weave(hashes(NV, 64)); vc(D("kmf"), D("kmi")); products(1)
+            weave(hashes(0, NV), lists(1))
+            sa(D("xr"), IND(D(XL, 0, NV), D("xo")), F.Copy)
+            products(0); weave(lists(0, 0, 4), lists(0, 4, 8))
         else:
-            lists(list(range(8))); slists()
+            sa(D("xr"), IND(D(XL, 0, NV), D("xo")), F.Copy)
+            weave(hashes(0, 64), own(t - 1))
+            products(1); products(0); rest(t - 1)
+            weave(lists(1), lists(0))
         nq = 2 if last else 4
         nk_ = 64 * nq
         np_ = nk_ if last else nk_ + 64
-
-        def strides():
-            vs(D("h31"), D("um"), 31, A.bitwise_and)
-            vs(D("hf"), D("h31"), 1.0, A.add)
 
         def steps():
             for k in range(4): sa(D("hp", 16 * k, 16 * k + 16), D("hf", (k + 1) % 4, 64, 4), F.Copy)
             for k in range(nq): sa(D("pw", k, nk_, nq), D("hp"), F.Identity, 0.0, D("qcol", k, k + 1))
             if not last: sa(D("pw", nk_, np_), D("hp"), F.Copy, 0.0, 63.0)
         n1 = 16 * NV
-        bank = ["pd0", "pd0", "pd1", "pu"]
-        at = [0, 2 * NV, 0, 0]
-        sbank = ["pds", "pds", "plf"]
-        scol = [0, 8 * SGR[0], 0]
+        bank = ["pd0", "pd1", "ppos", "pu"]
+        sbank = ["pds", "pw", "plf"]
         s0 = [sum(SGR[:c]) for c in range(4)]
+        sch = SCH[min(t, 1)]; ABS = ABSR[min(t, 1)]
 
-        def vgather(c):
-            for m in (2 * c, 2 * c + 1): vt(D("dv", m * n1, m * n1 + n1), IND(D(X), D("of", m * NV, m * NV + NV)), D("xr"), A.subtract)
+        def vgather(m): vt(D("dv", m * n1, m * n1 + n1), IND(D(X), D("of", m * NV, m * NV + NV)), D("xr"), A.subtract)
+
+        def relu(c):
             if c not in ABS: vs(D("av", 2 * c * n1, 2 * c * n1 + 2 * n1), D("dv", 2 * c * n1, 2 * c * n1 + 2 * n1), 0.0, A.max)
 
         def sgather(c):
-            for i in range(sum(SCH[:c]), sum(SCH[:c + 1])):
+            for i in range(sum(sch[:c]), sum(sch[:c + 1])):
                 sa(D("as", i * 128, i * 128 + 128), IND(D(X), D("of", SC + 8 * i, SC + 8 * i + 8)), F.Abs, D("nx", NV + i, NV + i + 1))
             if c in ABS: sa(D("av", 2 * c * n1, 2 * c * n1 + 2 * n1), D("dv", 2 * c * n1, 2 * c * n1 + 2 * n1), F.Abs)
 
@@ -323,42 +347,35 @@ def rank_program(g, core, T, topo):
 
         def vsums(c):
             n = 2 * NV; lo = 2 * c * n1; hi = lo + 2 * n1
-            o = D(bank[c], at[c], at[c] + n)
-            bias = [(D("nb"), D("ones", 0, n))]
-            if c in ABS: pe(o, bias + sums("sel", "av", lo, hi))
-            else: pe(o, bias + sums("seln", "dv", lo, hi), sums("sel2", "av", lo, hi))
+            o = D(bank[c], 0, n)
+            if c in ABS: pe(o, sums("sel", "av", lo, hi), start=False)
+            else: pe(o, sums("seln", "dv", lo, hi), sums("sel2", "av", lo, hi) + [(D("nb"), D("ones", 0, n))], start=False)
 
-        def ssums(q):
-            n = 8 * SGR[q]
-            pe(D(sbank[q], scol[q], scol[q] + n), [(D("nb"), D("ones", 0, n))] + sums("sel", "as", s0[q] * 128, s0[q + 1] * 128))
+        def ssums(q): pe(D(sbank[q], 0, 8 * SGR[q]), sums("sel", "as", s0[q] * 128, s0[q + 1] * 128), start=False)
+        for P, lo, n, b in [(bank[c], 2 * c * NV, 2 * NV, c in ABS) for c in range(4)] + [(sbank[q], SC + 8 * s0[q], 8 * SGR[q], True) for q in range(3)]:
+            pe(D(P, 0, n), [(D("idn"), D("cf", lo, lo + n))] + [(D("nb"), D("ones", 0, n))] * b, stop=False)
 
-        def posts(parts):
-            for P, b, lo, n, o in parts: vt(D("nk", lo, lo + n), D(P, b, b + n), D("ci", lo, lo + n), A.add)
-            for P, b, lo, n, o in parts: vt(D("pv", lo, lo + n), D(P, b, b + n), D("th4", lo, lo + n), A.is_lt)
-            for P, b, lo, n, o in parts: vt(o or D("pv", lo, lo + n), D("pv", lo, lo + n), D("nk", lo, lo + n), A.mult)
+        def keys(P, lo, n, first, least):
+            yield vt(D("nk", lo, lo + n), D(P, 0, n), D("th4", lo, lo + n), A.is_lt)
+            yield vt(D("tm0") if first else D("pv", lo, lo + n), D(P, 0, n), D("nk", lo, lo + n), A.mult)
+            yield least()
 
-        def smin(a, b): vscan(D("sm", 8 * a, 8 * b), D("s8", 8 * a, 8 * b), D("pv", SC + 8 * a, SC + 8 * b), 0.0, A.max, A.min)
+        def vkeys(c):
+            lo = 2 * c * NV
+            return keys(bank[c], lo, 2 * NV, c == 0, lambda: vt(D("tm0"), D("tm0"), D("pv", lo, lo + 2 * NV), A.min))
 
-        def vmin(c): vt(D("tm0"), D("tm0"), D("pv", 2 * c * NV, 2 * c * NV + 2 * NV), A.min)
-        vgather(0)
-        if t == 0: lists(list(range(2, 8)))
-        sgather(0)
-        vgather(1); vsums(0); sgather(1); ssums(0)
-        vgather(2); vsums(1); sgather(2); vsums(2); sgather(3)
-        vgather(3); vsums(3); ssums(1); ssums(2)
-        posts([("pd0", 0, 0, 4 * NV, D("mk")), ("pd1", 0, 4 * NV, 2 * NV, None)])
-        vt(D("tm0"), D("mk", 0, 2 * NV), D("mk", 2 * NV, 4 * NV), A.min)
-        strides(); vmin(2)
-        sa(D("dw"), D("c16"), F.Copy, 0.0, 0.0); steps()
-        posts([("pu", 0, 6 * NV, 2 * NV, None), ("pds", 0, SC, 8 * s0[2], None)]); vmin(3); smin(0, s0[2])
+        def skeys(q):
+            a, b = 8 * s0[q], 8 * s0[q + 1]
+            return keys(sbank[q], SC + a, b - a, False, lambda: vscan(D("sm", a, b), D("s8", a, b), D("pv", SC + a, SC + b), 0.0, A.max, A.min))
+        kv = [vkeys(c) for c in range(4)]; ks = [skeys(q) for q in range(3)]
+        calls = {"g": vgather, "r": relu, "p": vsums, "q": ssums, "c": sgather, "v": lambda a: next(kv[a]), "s": lambda a: next(ks[a])}
+        for step in ORDER.split(): calls[step[0]](int(step[1]))
         vt(D("bk", 0, NV), D("tm0", 0, NV), D("tm0", NV, 2 * NV), A.min)
-        if NV == 32: vx(D("t1", 0, 32), D("bk", 0, 32))
-        posts([("plf", 0, SC + 8 * s0[2], 8 * SGR[2], None)]); smin(s0[2], NS)
-        if NV == 32:
-            vx(D("t1", 32, 64), D("sm", 7, 8 * NS, 8))
-        else:
-            vc(D("bk", NV, 64), D("sm", 7, 8 * NS, 8)); vx(D("t1"), D("bk"))
+        vx(D("t1", 32, 64), D("sm", 7, 8 * NS, 8)); vx(D("t1", 0, 32), D("bk", 0, 32))
+        vs(D("h31"), D("um"), 31, A.bitwise_and)
         vscan(D("bsc"), D("s16"), D("t1"), 0.0, A.max, A.min)
+        vs(D("hf"), D("h31"), 1.0, A.add)
+        sa(D("dw"), D("th4", 0, 256), F.Copy, 0.0, 0.0); steps()
         vc(D("bi"), D("bsc", 15, 64, 16)); vt(D("t0"), D("bsc", 15, 64, 16), D("i64"), A.add)
         vs(D("jb64"), D("bi"), 4032, A.bitwise_and)
         vs(D("jf"), D("jb64"), 64.0, A.add); vt(D("tt1"), D("t0"), D("jb64"), A.subtract)
@@ -372,13 +389,8 @@ def rank_program(g, core, T, topo):
         vt(D("ai"), D("acs", 31, 128, 32), D("defn"), A.min); sa(D("got"), D("acs", 31, 128, 32), F.Sign, 0.0, -1.0)
         vs(D("pa"), D("ai"), 4032, A.bitwise_and, 6, A.logical_shift_right)
         vs(D("oh"), D("ai"), 62, A.bitwise_and, 1, A.logical_shift_right)
-        vc(D("pf"), D("pa"))
         for x in range(2): vt(D("pl", x, 8, 2), D("pa"), D("mm%d" % x), A.mult)
-        bs = (0, 2, 1, 3)
-        for c in range(4):
-            zo = D("z", 16 * c, 16 * c + 16); zi = D("pf", bs[c], bs[c] + 1)
-            if c < 2: sa(zo, D("z64", 0, 16), F.Identity, zi)
-            else: vs(zo, D("z64", 0, 16), zi, A.add)
+        vc(D("z"), IND(D("pa"), D("zl")))
         pe(D("plf", 0, 4), [(D("u0"), D("pl", 0, 4)), (D("u1"), D("pl", 4, 8))])
         vt(D("cut"), D("oh"), D("got"), A.add)
         vx(D("r1"), D("z")); vc(D("l1"), D("plf", 0, 4))
@@ -395,7 +407,7 @@ def rank_program(g, core, T, topo):
         vc(D("r3"), IND(D("r2"), L1))
         vt(D("rl"), IND(D("r3"), L1), D("mdg"), A.mult); sa(D("r4"), IND(D("r3"), L1), F.Copy)
         sa(D("l64"), D("pu", 0, 1), F.Copy, 0.0, 0.015625); sa(D("l8k"), D("pu", 0, 1), F.Copy, 0.0, 8192.0); sa(D("lcol"), D("pu", 0, 1), F.Copy)
-        for c in range(4): sa(D("zc", 16 * c, 16 * c + 16), D("z64", 0, 16), F.Identity, D("cut", bs[c], bs[c] + 1))
+        sa(D("zc"), IND(D("cut"), D("zl")), F.Copy)
         vscan(D("sl"), D("rst"), D("rl"), 0.0, A.mult, A.add)
         vc(L4, D("sl", 15, 64, 16))
         vs(D("sp"), D("kp"), D("l64"), A.mult, -0.4921875, A.add)
@@ -415,42 +427,36 @@ def rank_program(g, core, T, topo):
         vc(D("r32"), IND(D("r16"), L16))
         vx(D("cr"), D("zc"))
         vc(D("r48"), IND(D("r32"), L16))
-        vt(D("er"), D("cr"), D("ej"), A.add)
+        vt(D("pu", 64, 128), D("cr"), D("ej"), A.add); sa(D("pu", 128, 192), D("pu", 64, 128), F.Copy, 16.0)
         vt(D("rl3"), IND(D("r48"), L16), D("mdg"), A.mult)
         vt(D("kr"), IND(D("r48"), L16), D("jj"), A.add)
         vscan(D("sl3"), D("rst"), D("rl3"), 0.0, A.mult, A.add)
-        vs(D("ww"), D("kr"), 262144.0, A.mult)
         for q in range(4): vs(D("cc%d" % q), D("kr"), D("sl3", 16 * q + 15, 16 * q + 16), A.subtract, D("qj", q, q + 1), A.is_gt)
-        pe(D("ppos", 0, 64), [(D("lb%d" % q), D("cc%d" % q)) for q in range(4)])
+        pe(D("ppos", 0, 64), [(D("n75"), D("ones", 0, 64))], [(D("lb%d" % q), D("cc%d" % q)) for q in range(4)])
         vt(D("pq", 0, np_), D("pp", 0, np_), D("pv", 0, np_), A.subtract)
-        vt(D("pm"), D("ppos", 0, 64), D("mdg"), A.mult)
-        vc(D("pi"), D("ppos", 0, 64))
+        vt(D("pm"), D("ppos", 0, 64), D("md16"), A.mult)
+        vs(D("pi"), D("ppos", 0, 64), 7.5, A.add)
         vscan(D("ps"), D("rst"), D("pm"), 0.0, A.mult, A.add)
         vs(D("pr"), D("pi"), 15, A.bitwise_and)
-        vt(D("ew"), D("er"), D("ww"), A.add)
-        vs(D("tl4"), D("ps", 15, 64, 16), 0.0625, A.mult, -0.46875, A.add)
-        vt(D("vvv"), D("ew"), D("pr"), A.subtract); vs(D("mlt"), D("pr"), D("rcol"), A.is_le)
-        vc(D("tl", 0, 4), D("tl4")); vs(D("tl", 4, 8), D("tl4"), 1.0, A.add)
-        vt(D("vv", 0, 64), D("vvv"), D("mlt"), A.mult); sa(D("vv", 64, 128), D("vvv"), F.Copy, 16.0)
+        for e in range(2): vs(D("tl", 4 * e, 4 * e + 4), D("ps", 15, 64, 16), float(ROUND), A.add, float(e - ROUND), A.add)
+        vs(D("mlt", 0, 64), D("pr"), D("rcol"), A.is_le)
+        for e in range(2): vt(D("vv", 64 * e, 64 * e + 64), D("pu", 64 * e + 64, 64 * e + 128), D("pr"), A.subtract)
+        vt(IND(D("dw"), D("tl")), D("vv"), D("mlt"), A.mult)
         if not last: vt(D("lm"), D("pq", nk_, np_), D("mdg"), A.mult)
-        vc(IND(D("dw"), D("tl")), D("vv"))
-        if not last: vscan(D("lsc"), D("rst"), D("lm"), 0.0, A.mult, A.add)
-        vscan(D("ls", 0, LAY0), D("c16", 0, LAY0), D("dw", 0, LAY0), -1000.0, A.add, A.max)
-        if not last: vc(D("lx"), D("lsc", 15, 64, 16))
-        vc(D("lsi", 0, LAY0), D("ls", 0, LAY0))
-        vscan(D("ls", LAY0, 256), D("c16", LAY0, 256), D("dw", LAY0, 256), D("ls", LAY0 - 1, LAY0), A.add, A.max)
-        vs(D("lsa", 0, LAY0), D("lsi", 0, LAY0), 4095, A.bitwise_and)
-        vc(D("lsi", LAY0, 256), D("ls", LAY0, 256))
-        vc(D("lay", 0, LAY0), D("lsa", 0, LAY0))
-        vs(D("lsa", LAY0, 256), D("lsi", LAY0, 256), 4095, A.bitwise_and)
+        for lo, hi in ((0, LAY0), (LAY0, 256)): sa(D("dk", lo, hi), D("dw", lo, hi), F.Copy, 16.0, -65536.0)
         vc(D("kl", 0, nk_), D("pq", 0, nk_))
-        vc(D("lay", LAY0, 256), D("lsa", LAY0, 256))
+        vscan(D("ls", 0, LAY0), D("dk", 0, LAY0), D("dw", 0, LAY0), 0.0, A.add, A.max)
+        if not last: vscan(D("lsc"), D("rst"), D("lm"), 0.0, A.mult, A.add)
+        vs(D("lay", 0, LAY0), D("ls", 0, LAY0), -32.0, A.add, 4095.0, A.min)
+        vscan(D("ls", LAY0, 256), D("dk", LAY0, 256), D("dw", LAY0, 256), D("ls", LAY0 - 1, LAY0), A.add, A.max)
+        if not last: vc(D("lx"), D("lsc", 15, 64, 16))
+        vs(D("lay", LAY0, 256), D("ls", LAY0, 256), -32.0, A.add, 4095.0, A.min)
         sa(D("xp", 0, 16 * LAY0), IND(D(X), D("lay", 0, LAY0)), F.Copy)
         sa(D("xp", 16 * LAY0, 16 * LAYS[t]), IND(D(X), D("lay", LAY0, LAYS[t])), F.Copy)
         vc(D("xp", 16 * LAYS[t], 4096), IND(D(X), D("lay", LAYS[t], 256)))
         w = WIDTH[t]
-        n = w // 32
-        if not last:
+
+        def ahead():
             XK = "xk%d" % t; XLN = "xl%d" % (t + 1)
             vc(D(XK), IND(D("xp"), D("lx")))
             sync_for("g", [], D(XK, 0, 48)[1])
@@ -464,19 +470,20 @@ def rank_program(g, core, T, topo):
             g.remote_dma_fused(trs, local_sem=T.sem.tx)
             sent[0] += 6
             source("XS%d" % (t + 1), "xs%d" % (t + 1), 6, [(XLN, 16 * p, 16 * p + 16, 1) for p in range(n_ranks) if p != rank])
-        for k in range(4):
-            buf, o = (SRC[t], k * w) if k < 3 else (DST[t], rank * w)
-            vc(D(buf, o, o + w // 2), IND(D("xp"), D("kl", 2 * k * n, 2 * k * n + n)))
-            sa(D(buf, o + w // 2, o + w), IND(D("xp"), D("kl", 2 * k * n + n, 2 * k * n + 2 * n)), F.Copy)
-            if k < 3: send(t, k)
-        if not last:
             vc(D(XLN, 16 * rank, 16 * rank + 16), D(XK, 48, 64))
-            for k in range(3): arrival(t, k)
+
+        def kids(buf, o, a, n):
+            vc(D(buf, o, o + n // 2), IND(D("xp"), D("kl", a // 16, a // 16 + n // 32)))
+            sa(D(buf, o + n // 2, o + n), IND(D("xp"), D("kl", a // 16 + n // 32, a // 16 + n // 16)), F.Copy)
+        for i, k, lo, on, by, h in pieces(t):
+            kids(SRC[t], k * w + lo, k * w + lo, on + by); send(t, i, k, lo, on, by, h)
+            if i == 0 and not last: ahead()
+        if last: kids(DST[t], rank * w, 3 * w, w)
 
     for k in range(4):
         p = rank if k == 0 else arrival(2, k - 1)
-        sync_for("y", [], D("yb", p * 512, p * 512 + 512)[1])
-        g.sync.dma_start(T.y[:, p * 512:p * 512 + 512], T.yb[:, p * 512:p * 512 + 512]).then_inc(T.sem.stor, 16)
+        sync_for("ys"[k % 2], [], D("yb", p * 512, p * 512 + 512)[1])
+        queue["ys"[k % 2]].dma_start(T.y[:, p * 512:p * 512 + 512], T.yb[:, p * 512:p * 512 + 512]).then_inc(T.sem.stor, 16)
     g.sync.wait_ge(T.sem.stor, 64)
     g.wait_ge(T.sem.tx, sent[0])
     for q in ("v", "s", "t", "g"):

from concourse.bass import DstId, RemoteDMATransfer
from concourse.mybir import dt, AluOpType as A, AxisListType, ActivationFunctionType as F

NV = 32
NS = 64 - NV
SCH = ([16, 4, 4, 8], [8, 6, 10, 8])
SGR = [12, 12, 8]
ABSR = ((0, 1), (0,))
ORDER = "g0 g1 g2 c0 g3 p0 g4 r1 c1 p1 q0 g5 v0 g6 r2 p2 v0 v1 c2 q1 g7 v1 s0 r3 p3 c3 q2 v1 s0 v2 s0 v2 s1 v2 s1 v3 s1 s2 v3 s2 v3 s2"
WIDTH = (1024, 1024, 512)
_MID = ((0, 256, 256, 0), (0, 256, 256, 1), (1, 512, 512, 2), (2, 896, 128, 3))
PLAN = (_MID, _MID, ((0, 256, 256, 0), (1, 256, 256, 1), (2, 512, 0, 0)))
LAYS = (138, 138, 138)
LAY0 = 64
OWNV = 6
BIG = 16777216
ROUND = 12582912
SC = NV * 8

_F32 = [("wtf", 1), ("kmf", 24), ("thf", 8), ("mdg", 64), ("rst", 64), ("rcol", 1), ("qcol", 4), ("qj", 4), ("iq", 4), ("i64", 4), ("ib", 4), ("idf", 4), ("df", 4), ("defn", 4),
        ("s16", 64), ("s32", 128), ("s8", 8 * NS), ("j64", 64), ("jp", 64), ("jm0", 64), ("jm1", 64), ("ej", 64), ("jj", 64), ("z64", 64), ("m0", 1), ("m1", 1), ("mm0", 4), ("mm1", 4),
        ("kp", 64), ("th4", 512),
        ("nx", 64), ("uf", 64), ("uk", 512), ("nk", 512), ("tm0", 2 * NV), ("sm", 8 * NS),
        ("bk", 64), ("t1", 64), ("bsc", 64), ("t0", 4), ("jf", 4), ("tt1", 4),
        ("pm0", 128), ("px", 128), ("t2", 128), ("acs", 128), ("got", 4), ("cut", 4), ("z", 64), ("zc", 64), ("r1", 64), ("cr", 64), ("md16", 64),
        ("r2", 64), ("r3", 64), ("r4", 64), ("rl", 64), ("sl", 64), ("r8", 64), ("r12", 64), ("r16", 64), ("rl2", 64), ("sl2", 64), ("r32", 64), ("r48", 64),
        ("kr", 64), ("rl3", 64), ("sl3", 64), ("lenl", 4), ("pm", 64), ("ps", 64), ("mlt", 128), ("vv", 128),
        ("r32c", 1), ("cf", 512), ("idn", 128), ("one", 128), ("dk", 256), ("dw", 256), ("ls", 256), ("hf", 64), ("hp", 64), ("lcol", 1), ("l64", 1), ("l8k", 1), ("pp", 320), ("wa", 320), ("pq", 320), ("lm", 64), ("lsc", 64)]
_I32 = [("wti", 1), ("kmi", 24), ("thi", 8), ("icc", 1), ("id4", 4), ("ixo", NV + 4), ("iu", 128), ("ui", 64), ("um", 64), ("uu", 64), ("vi", 64),
        ("cp", 512), ("ci", 512), ("bi", 4), ("jb64", 4), ("ai", 4), ("pa", 4), ("oh", 4), ("pi", 64), ("pr", 64), ("lsi", 128),
        ("h31", 64), ("sp", 64)]
_BF = [("xa", 4096), ("xb", 4096), ("xl0", 64), ("xl1", 64), ("xl2", 64), ("xp", 4096), ("kb0", 3072), ("kb1", 3072), ("kb2", 1536), ("yb", 2048),
       ("xk0", 64), ("xk1", 64), ("ones", 128), ("bt", 128), ("blk", 128), ("wb", 128), ("sel", 144), ("sel2", 144), ("seln", 144), ("nb", 128), ("n75", 128),
       ("u0", 128), ("u1", 128), ("b32", 128), ("b3t", 128), ("wm", 128), ("wm2", 128), ("lb0", 128), ("lb1", 128), ("lb2", 128), ("lb3", 128),
       ("xr", 16 * NV), ("dv", 128 * NV), ("av", 128 * NV), ("as", 128 * NS),
       ("pl", 8), ("cl", 8), ("lenb", 4), ("cc0", 64), ("cc1", 64), ("cc2", 64), ("cc3", 64)]
_U16 = [("xo", NV), ("of", 512), ("l1", 4), ("l4", 4), ("l16", 4), ("tl", 8), ("lay", 256), ("kl", 256), ("lx", 4), ("zl", 4)]
_PS = ["pu", "pd0", "pd1", "pds", "pv", "plf", "ppos", "pw"]
_OWN = ("xa", "xb", "xl0", "xl1", "xl2", "kb0", "kb1", "kb2", "yb", "xk0", "xk1", "wti", "kmi", "thi")
SCRATCH = {}
PLACE = {}
for _l, _d, _b, _al in ((_F32, "float32", "ff", 8), (_I32, "int32", "ii", 8), (_BF, "bfloat16", "bb", 16), (_U16, "uint16", "uh", 16)):
    _at = 0
    for _n, _w in _l:
        if _n in _OWN:
            SCRATCH[_n] = ("sbuf", [128, _w], _d); PLACE[_n] = (_n, 0, _w)
        else:
            PLACE[_n] = (_b, _at, _w); _at += (_w + _al - 1) // _al * _al
    SCRATCH[_b] = ("sbuf", [128, _at], _d)
for _n in _PS:
    SCRATCH[_n] = ("psum", [128, 512], "float32"); PLACE[_n] = (_n, 0, 512)
SEMAPHORES = ["sv", "ss", "st", "sg", "lw", "lk", "lt", "lx0", "lx1", "xs1", "xs2", "stor", "tx"]
SEMAPHORES += ["ar%d_%d" % (t, k) for t in range(3) for k in range(3)] + ["ra%d_%d" % (t, i) for t in range(3) for i in range(len(PLAN[t]))]


def rank_program(g, core, T, topo):
    n_ranks = len(T.cores)
    SRC = ("kb0", "kb1", "kb2"); DST = ("xb", "xa", "yb")

    def helpers(rc):
        return [c for c in topo.cores_of(rc) if topo.die(c) != topo.die(rc) and all(topo.may_write(c, d) for d in T.cores)]

    def hop_engines(rc, hc, d):
        off = topo.engines(rc, d)
        return [e for e in topo.engines(rc, hc) if e not in off]

    def pieces(t):
        at = [0, 0, 0]
        for i, (k, on, by, h) in enumerate(PLAN[t]):
            yield i, k, at[k], on, by, h
            at[k] += on + by
    rank = T.rank_of(core)
    if rank is None:
        for r, rc in enumerate(T.cores):
            hs = helpers(rc)
            if core not in hs: continue
            n = 0
            for t in range(3):
                for i, k, lo, on, by, h in pieces(t):
                    if not by or hs[h] != core: continue
                    d = T.cores[(r + k + 1) % n_ranks]
                    rid, pid = topo.addr(d, core)
                    w = WIDTH[t]; a = lo + on
                    g.wait_ge(T.sem["ra%d_%d" % (t, i)], len(hop_engines(rc, core, d)))
                    g.remote_dma(T[DST[t]][:, r * w + a:r * w + a + by], T[SRC[t]][:, k * w + a:k * w + a + by], T.sem["ar%d_%d" % (t, k)], T.sem.tx, pid, rid, topo.mask(core, d))
                    n += len(topo.engines(core, d))
            if n: g.wait_ge(T.sem.tx, n)
        return
    queue = {"v": g.vector, "s": g.scalar, "t": g.tensor, "g": g, "y": g.sync}
    semname = {"v": "sv", "s": "ss", "t": "st", "g": "sg"}
    count = {"v": 0, "s": 0, "t": 0, "g": 0}
    value = {}
    known = {q: {} for q in queue}
    snap = {}
    sent = [0]
    log = {}

    def D(n, lo=0, hi=None, st=1, p=(0, 128)):
        b, at, w = PLACE[n]
        if hi is None: hi = w
        hi = min(hi, w)
        return (T[b][p[0]:p[1], at + lo:at + hi] if st == 1 else T[b][p[0]:p[1], at + lo:at + hi:st], [(n, lo, hi, st)])

    def IND(win, off):
        return (win[0].indirect(off[0]), win[1] + off[1])

    def meet(a, b):
        if a[0] >= b[1] or b[0] >= a[1]: return False
        return not (a[2] == b[2] and a[2] > 1 and (a[0] - b[0]) % a[2] != 0)

    def sync_for(q, outs, ins):
        need = {}
        for w, keys in ((True, outs), (False, ins)):
            for (n, lo, hi, st) in keys:
                ps = SCRATCH[PLACE[n][0]][0] == "psum"
                for (src, w2, lo2, hi2, st2), k in log.get(n, {}).items():
                    hit = (ps and src != q) or ((w or w2) and meet((lo, hi, st), (lo2, hi2, st2)))
                    if hit and need.get(src, 0) < k: need[src] = k
        for src, k in need.items():
            wait(q, src, k)

    def wait(q, src, k):
        if known[q].get(src, 0) >= k: return
        queue[q].wait_ge(T.sem[semname[src]], value[(src, k)])
        for s2, k2 in list(snap[(src, k)].items()) + [(src, k)]:
            if known[q].get(s2, 0) < k2: known[q][s2] = k2

    def note(src, k, outs, ins):
        for w, keys in ((True, outs), (False, ins)):
            for (n, lo, hi, st) in keys:
                log.setdefault(n, {})[(src, w, lo, hi, st)] = k

    def done(q, ins_):
        count[q] += 1
        ins_.then_inc(T.sem[semname[q]], 1)
        value[(q, count[q])] = count[q]
        snap[(q, count[q])] = dict(known[q])
        return count[q]

    def source(name, sem, val, outs):
        semname[name] = sem
        value[(name, 1)] = val
        snap[(name, 1)] = {}
        note(name, 1, outs, [])

    def col(x):
        return (x[0], x[1]) if isinstance(x, tuple) else (x, [])

    def run(q, o, i, make):
        sync_for(q, o[1], i)
        note(q, done(q, make()), o[1], i)

    def vt(o, a, b, op): run("v", o, a[1] + b[1], lambda: g.vector.tensor_tensor(o[0], a[0], b[0], op))

    def vs(o, a, s1, op0, s2=None, op1=None):
        c1, k1 = col(s1); c2, k2 = col(s2)
        if op1 is None: run("v", o, a[1] + k1, lambda: g.vector.tensor_scalar(o[0], a[0], c1, None, op0))
        else: run("v", o, a[1] + k1 + k2, lambda: g.vector.tensor_scalar(o[0], a[0], c1, c2, op0, op1))

    def vc(o, a): run("v", o, a[1], lambda: g.vector.tensor_copy(o[0], a[0]))

    def vm(o, c): run("v", o, [], lambda: g.vector.memset(o[0], c))

    def vscan(o, a, b, init, op0, op1):
        c1, k1 = col(init)
        run("v", o, a[1] + b[1] + k1, lambda: g.vector.tensor_tensor_scan(o[0], a[0], b[0], c1, op0, op1))

    def vx(o, a): run("v", o, a[1], lambda: g.vector.transpose(o[0], a[0]))

    def sa(o, a, f, bias=0.0, scale=1.0):
        c1, k1 = col(bias); c2, k2 = col(scale)
        run("s", o, a[1] + k1 + k2, lambda: g.scalar.activation(o[0], a[0], f, bias=c1, scale=c2))

    def pe(o, *parts, start=True, stop=True):
        i = []
        r = None
        for p, pairs in enumerate(parts):
            j = [k for a, b in pairs for k in a[1] + b[1]]
            sync_for("t", o[1] if p == 0 and start else [], j)
            i = i + j
            for n, (a, b) in enumerate(pairs):
                r = g.tensor.matmul(o[0], a[0], b[0], start and p == 0 and n == 0, stop and p == len(parts) - 1 and n == len(pairs) - 1)
        note("t", done("t", r), o[1], i)

    def gi(o, pattern, base, cm):
        if SCRATCH[PLACE[o[1][0][0]][0]][2] == "int32": run("g", o, [], lambda: g.iota(o[0], pattern, base, cm))
        else: run("g", o, [], lambda: g.iota(o[0], pattern, base, cm, allow_small_or_imprecise_dtypes=True))

    def gsel(o, a, pattern, op, base, cm): run("g", o, a[1], lambda: g.affine_select(o[0], a[0], pattern, op, 0.0, base, cm))

    def load(q, sem, o, src):
        queue[q].dma_start(o[0], src).then_inc(T.sem[sem], 16)
        source(sem, sem, 16, o[1])

    def send(t, i, k, lo, on, by, h):
        d = T.cores[(rank + k + 1) % n_ranks]
        rid, pid = topo.addr(d, core)
        w = WIDTH[t]; a = k * w + lo; m = a + on
        S = T[SRC[t]]
        sync_for("g", [], D(SRC[t], a, m + by)[1])
        trs = []
        if by:
            hc = helpers(core)[h]
            hrid, hpid = topo.addr(hc, core)
            he = hop_engines(core, hc, d)
            trs.append(RemoteDMATransfer(dst_ids=[DstId(rid=hrid, pnc=hpid)], dma_engine_mask=sum(1 << e for e in he), remote_sem=T.sem["ra%d_%d" % (t, i)], src=S[:, m:m + by], dst=S[:, m:m + by]))
            sent[0] += len(he)
        if on:
            trs.append(RemoteDMATransfer(dst_ids=[DstId(rid=rid, pnc=pid)], dma_engine_mask=topo.mask(core, d), remote_sem=T.sem["ar%d_%d" % (t, k)], src=S[:, a:m], dst=T[DST[t]][:, rank * w + lo:rank * w + lo + on]))
            sent[0] += len(topo.engines(core, d))
        for call in ([trs] if on == by else [[x] for x in trs]): g.remote_dma_fused(call, local_sem=T.sem.tx)

    def arrival(t, k):
        p = (rank - k - 1) % n_ranks
        cnt = sum((len(topo.engines(T.cores[p], core)) if on else 0) + (len(topo.engines(helpers(T.cores[p])[h], core)) if by else 0) for i, k2, lo, on, by, h in pieces(t) if k2 == k)
        source("AR%d_%d" % (t, k), "ar%d_%d" % (t, k), cnt, D(DST[t], p * WIDTH[t], (p + 1) * WIDTH[t])[1])
        return p

    def own(t):
        yield None
        for a in range(0, 4 * OWNV, OWNV):
            yield vc(D(DST[t], rank * 1024 + 16 * a, rank * 1024 + 16 * (a + OWNV)), IND(D("xp"), D("kl", 192 + a, 192 + a + OWNV)))

    def rest(t):
        sa(D(DST[t], rank * 1024 + 64 * OWNV, rank * 1024 + 1024), IND(D("xp"), D("kl", 192 + 4 * OWNV, 256)), F.Copy)
        for k in range(3): arrival(t, k)

    def weave(*gs):
        for _ in range(6):
            for x in gs: next(x, None)

    load("y", "lx0", D("xa", 64 * NV, 4096), T.gen0[:, 64 * NV:4096])
    load("s", "lw", D("wti"), T.wt[:]); load("s", "lt", D("thi"), T.th[:])
    load("y", "lx1", D("xa", 0, 64 * NV), T.gen0[:, 0:64 * NV])
    load("s", "lk", D("kmi"), T.km[:])

    vm(D("ones"), 1.0); vm(D("sel"), 0.0)
    gi(D("icc"), [[0, 1]], 0, 1); gi(D("iu"), [[1, 128]], 128, -1)
    gsel(D("bt"), D("ones"), [[-16, 8], [0, 16]], A.is_ge, 0, 1)
    gsel(D("b3t"), D("ones"), [[-32, 4], [0, 32]], A.is_ge, 0, 1)
    gsel(D("blk"), D("bt"), [[16, 8], [0, 16]], A.is_ge, 15, -1)
    gsel(D("b32"), D("b3t"), [[32, 4], [0, 32]], A.is_ge, 31, -1)
    gi(D("id4"), [[0, 4]], 0, 64); gi(D("ib"), [[2048, 2], [0, 2]], 0, 0); gi(D("idf"), [[0, 2], [2048, 2]], 0, 0)
    gi(D("ixo", 0, NV), [[1, NV]], 0, 0); gi(D("ixo", NV, NV + 4), [[1, 2], [2, 2]], 0, 0)
    gi(D("j64"), [[64, 64]], 0, 0); gi(D("iq"), [[16, 4]], 0, 0)
    vm(D("z64"), 0.0); vm(D("nb"), -131072.0); vm(D("n75"), -7.5 / 128); vm(D("one"), 1.0); vm(D("mlt", 64, 128), 1.0); vm(D("rst"), 1.0)
    vm(D("s32"), float(-2 * BIG)); vm(D("s8"), float(-2 * BIG)); vm(D("s16"), float(-2 * BIG))
    vm(D("s32", 0, 128, 32), 1.0); vm(D("s8", 0, 8 * NS, 8), 1.0); vm(D("s16", 0, 64, 16), 1.0); vm(D("rst", 0, 64, 16), 0.0)
    vs(D("pi", 0, 1), D("icc"), 15, A.bitwise_and); vs(D("pr", 0, 1), D("icc"), 4, A.logical_shift_right, 1, A.bitwise_and)
    vs(D("lsi"), D("iu"), 15, A.bitwise_and)
    vc(D("rcol"), D("pi", 0, 1)); vc(D("m1"), D("pr", 0, 1))
    vs(D("wm"), D("lsi"), 0.0, A.is_equal); vs(D("mdg"), D("lsi", 0, 64), 0.0, A.is_equal); vs(D("md16"), D("lsi", 0, 64), 0.0, A.is_equal, 0.0625, A.mult)
    vs(D("sel", 15, 143, 16), D("blk", 0, 128, 16), 4096.0, A.mult)
    vc(D("wtf"), D("wti"))
    vt(D("wm2"), D("wm"), D("b32"), A.mult)
    vs(D("wb"), D("blk"), D("wtf"), A.mult)
    vs(D("bi"), D("id4"), 2047, A.bitwise_and)
    vc(D("xo"), D("ixo", 0, NV)); vc(D("zl"), D("ixo", NV, NV + 4))
    vt(D("i64"), D("bi"), D("ib"), A.add); vt(D("df"), D("bi"), D("idf"), A.add)
    vs(D("defn"), D("df"), -4096.0, A.add)
    vs(D("thf"), D("thi"), 4096.0, A.mult, float(-BIG), A.add)
    sa(D("m0"), D("m1"), F.Copy, 1.0, -1.0); sa(D("r32c"), D("rcol"), F.Copy, 32.0)
    sa(D("sel2"), D("sel"), F.Copy, 0.0, 2.0); sa(D("seln"), D("sel"), F.Copy, 0.0, -1.0)
    sa(D("mm1"), D("z64", 0, 4), F.Identity, D("m1")); sa(D("mm0"), D("z64", 0, 4), F.Identity, D("m0"))
    sa(D("jj"), D("j64"), F.Copy, 0.0, 1.0 / 4096); sa(D("ej"), D("j64"), F.Identity, D("r32c"))
    sa(D("qcol"), D("iq"), F.Identity, D("rcol")); sa(D("qj"), D("qcol"), F.Copy, 0.0, 0.015625)
    for m in range(8):
        sa(D("th4", m * NV, m * NV + NV), D("z64", 0, NV), F.Identity, D("thf", m, m + 1))
        sa(D("th4", SC + m, 512, 8), D("z64", 0, NS), F.Identity, D("thf", m, m + 1))
    gsel(D("idn"), D("one"), [[-1, 128]], A.is_equal, 0, 1)
    gsel(D("u0"), D("wm2"), [[0, 4], [1, 2], [0, 16]], A.is_equal, 0, 0)
    gsel(D("u1"), D("wm2"), [[0, 4], [1, 2], [0, 16]], A.is_gt, 0, 0)
    gi(D("kp", 0, 48), [[1, 3], [4, 16]], 1, 0); gi(D("kp", 48, 64), [[4, 16]], 0, 0)
    gi(D("jp"), [[64, 64]], 64, 0)
    for b in range(2):
        for a in range(4):
            wait("g", "g", count["g"])
            gsel(D("jm%d" % b, p=(32 * a, 32 * a + 32)), D("jp", p=(32 * a, 32 * a + 32)), [[1, 64]], A.is_gt, -32 * b, -1)

    for t in range(3):
        last = t == 2
        X = "xb" if t == 1 else "xa"
        XL = "xl%d" % t

        def times(o, lo, hi, m):
            k = D("kmf", t * 8 + m, t * 8 + m + 1)
            if lo == 0 and t == 0: vs(o, D("um", lo, hi), k, A.mult)
            else: sa(o, D("uf", lo, hi), F.Identity, 0.0, k)

        def row(n, e, m):
            return D(n, SC + m, 512, 8) if e else D(n, m * NV, m * NV + NV)

        def products(e):
            if e: sa(D("nx", NV, 64), D(XL, NV, 64), F.Copy, 0.0, -1.0)
            for m in range(8): times(row("uk", e, m), NV * e, 64 if e else NV, m)

        def lists(e, m0=0, m1=8):
            lo, hi = (SC, 512) if e else (m0 * NV, m1 * NV)
            yield [vt(row("cp", e, m), row("uk", e, m), D("vi", NV * e, 64 if e else NV), A.add) for m in range(m0, m1)]
            yield vs(D("ci", lo, hi), D("cp", lo, hi), 4095, A.bitwise_and)
            yield vc(D("of", lo, hi), D("ci", lo, hi))
            yield vc(D("cf", lo, hi), D("ci", lo, hi))
        def hashes(lo, hi):
            if t == 0: vc(D(XL, lo, hi), D(X, 64 * lo + 63, 64 * hi, 64))
            yield pe(D("pu", lo, hi), [(D("wb"), D(XL, lo, hi))])
            yield vc(D("ui", lo, hi), D("pu", lo, hi))
            yield vs(D("um", lo, hi), D("ui", lo, hi), 4095, A.bitwise_and)
            if t or lo: vc(D("uf", lo, hi), D("um", lo, hi))
            yield vt(D("uu", lo, hi), D("um", lo, hi), D("um", lo, hi), A.mult)
            yield vs(D("vi", lo, hi), D("uu", lo, hi), 5, A.logical_shift_right)
        if t == 0:
            weave(hashes(NV, 64)); vc(D("kmf"), D("kmi")); products(1)
            weave(hashes(0, NV), lists(1))
            sa(D("xr"), IND(D(XL, 0, NV), D("xo")), F.Copy)
            products(0); weave(lists(0, 0, 4), lists(0, 4, 8))
        else:
            sa(D("xr"), IND(D(XL, 0, NV), D("xo")), F.Copy)
            weave(hashes(0, 64), own(t - 1))
            products(1); products(0); rest(t - 1)
            weave(lists(1), lists(0))
        nq = 2 if last else 4
        nk_ = 64 * nq
        np_ = nk_ if last else nk_ + 64

        def steps():
            for k in range(4): sa(D("hp", 16 * k, 16 * k + 16), D("hf", (k + 1) % 4, 64, 4), F.Copy)
            for k in range(nq): sa(D("pw", k, nk_, nq), D("hp"), F.Identity, 0.0, D("qcol", k, k + 1))
            if not last: sa(D("pw", nk_, np_), D("hp"), F.Copy, 0.0, 63.0)
        n1 = 16 * NV
        bank = ["pd0", "pd1", "ppos", "pu"]
        sbank = ["pds", "pw", "plf"]
        s0 = [sum(SGR[:c]) for c in range(4)]
        sch = SCH[min(t, 1)]; ABS = ABSR[min(t, 1)]

        def vgather(m): vt(D("dv", m * n1, m * n1 + n1), IND(D(X), D("of", m * NV, m * NV + NV)), D("xr"), A.subtract)

        def relu(c):
            if c not in ABS: vs(D("av", 2 * c * n1, 2 * c * n1 + 2 * n1), D("dv", 2 * c * n1, 2 * c * n1 + 2 * n1), 0.0, A.max)

        def sgather(c):
            for i in range(sum(sch[:c]), sum(sch[:c + 1])):
                sa(D("as", i * 128, i * 128 + 128), IND(D(X), D("of", SC + 8 * i, SC + 8 * i + 8)), F.Abs, D("nx", NV + i, NV + i + 1))
            if c in ABS: sa(D("av", 2 * c * n1, 2 * c * n1 + 2 * n1), D("dv", 2 * c * n1, 2 * c * n1 + 2 * n1), F.Abs)

        def sums(s, b, lo, hi):
            return [(D(s, 15 - r, 143 - r), D(b, lo + r, hi, 16)) for r in range(16)]

        def vsums(c):
            n = 2 * NV; lo = 2 * c * n1; hi = lo + 2 * n1
            o = D(bank[c], 0, n)
            if c in ABS: pe(o, sums("sel", "av", lo, hi), start=False)
            else: pe(o, sums("seln", "dv", lo, hi), sums("sel2", "av", lo, hi) + [(D("nb"), D("ones", 0, n))], start=False)

        def ssums(q): pe(D(sbank[q], 0, 8 * SGR[q]), sums("sel", "as", s0[q] * 128, s0[q + 1] * 128), start=False)
        for P, lo, n, b in [(bank[c], 2 * c * NV, 2 * NV, c in ABS) for c in range(4)] + [(sbank[q], SC + 8 * s0[q], 8 * SGR[q], True) for q in range(3)]:
            pe(D(P, 0, n), [(D("idn"), D("cf", lo, lo + n))] + [(D("nb"), D("ones", 0, n))] * b, stop=False)

        def keys(P, lo, n, first, least):
            yield vt(D("nk", lo, lo + n), D(P, 0, n), D("th4", lo, lo + n), A.is_lt)
            yield vt(D("tm0") if first else D("pv", lo, lo + n), D(P, 0, n), D("nk", lo, lo + n), A.mult)
            yield least()

        def vkeys(c):
            lo = 2 * c * NV
            return keys(bank[c], lo, 2 * NV, c == 0, lambda: vt(D("tm0"), D("tm0"), D("pv", lo, lo + 2 * NV), A.min))

        def skeys(q):
            a, b = 8 * s0[q], 8 * s0[q + 1]
            return keys(sbank[q], SC + a, b - a, False, lambda: vscan(D("sm", a, b), D("s8", a, b), D("pv", SC + a, SC + b), 0.0, A.max, A.min))
        kv = [vkeys(c) for c in range(4)]; ks = [skeys(q) for q in range(3)]
        calls = {"g": vgather, "r": relu, "p": vsums, "q": ssums, "c": sgather, "v": lambda a: next(kv[a]), "s": lambda a: next(ks[a])}
        for step in ORDER.split(): calls[step[0]](int(step[1]))
        vt(D("bk", 0, NV), D("tm0", 0, NV), D("tm0", NV, 2 * NV), A.min)
        vx(D("t1", 32, 64), D("sm", 7, 8 * NS, 8)); vx(D("t1", 0, 32), D("bk", 0, 32))
        vs(D("h31"), D("um"), 31, A.bitwise_and)
        vscan(D("bsc"), D("s16"), D("t1"), 0.0, A.max, A.min)
        vs(D("hf"), D("h31"), 1.0, A.add)
        sa(D("dw"), D("th4", 0, 256), F.Copy, 0.0, 0.0); steps()
        vc(D("bi"), D("bsc", 15, 64, 16)); vt(D("t0"), D("bsc", 15, 64, 16), D("i64"), A.add)
        vs(D("jb64"), D("bi"), 4032, A.bitwise_and)
        vs(D("jf"), D("jb64"), 64.0, A.add); vt(D("tt1"), D("t0"), D("jb64"), A.subtract)
        for b in range(2):
            for s in range(2):
                c = 2 * b + s
                vs(D("pm0", 64 * s, 64 * s + 64) if b == 0 else D("pv", 64 * s, 64 * s + 64), D("jm%d" % b), D("jf", c, c + 1), A.is_equal, D("tt1", c, c + 1), A.mult)
        vt(D("px"), D("pm0"), D("pv", 0, 128), A.min)
        vx(D("t2"), D("px"))
        vscan(D("acs"), D("s32"), D("t2"), 0.0, A.max, A.min)
        vt(D("ai"), D("acs", 31, 128, 32), D("defn"), A.min); sa(D("got"), D("acs", 31, 128, 32), F.Sign, 0.0, -1.0)
        vs(D("pa"), D("ai"), 4032, A.bitwise_and, 6, A.logical_shift_right)
        vs(D("oh"), D("ai"), 62, A.bitwise_and, 1, A.logical_shift_right)
        for x in range(2): vt(D("pl", x, 8, 2), D("pa"), D("mm%d" % x), A.mult)
        vc(D("z"), IND(D("pa"), D("zl")))
        pe(D("plf", 0, 4), [(D("u0"), D("pl", 0, 4)), (D("u1"), D("pl", 4, 8))])
        vt(D("cut"), D("oh"), D("got"), A.add)
        vx(D("r1"), D("z")); vc(D("l1"), D("plf", 0, 4))
        L1 = D("l1"); L4 = D("l4"); L16 = D("l16")

        def places(k):
            if k < nq: vt(D("pp", k, nk_, nq), D("pw", k, nk_, nq), D("sp"), A.add)
            elif not last: vt(D("pp", nk_, np_), D("pw", nk_, np_), D("sp"), A.add)
        for x in range(2): sa(D("cl", x, 8, 2), D("cut"), F.Identity, 0.0, D("m%d" % x))
        pe(D("plf", 4, 8), [(D("u0"), D("cl", 0, 4)), (D("u1"), D("cl", 4, 8))])
        vc(D("r2"), IND(D("r1"), L1))
        sa(D("lenb"), D("plf", 4, 8), F.Copy, 64.0, -1.0); sa(D("lenl"), D("plf", 4, 8), F.Copy, 64.0, -1.0)
        pe(D("pu", 0, 1), [(D("blk"), D("lenb", q, q + 1)) for q in range(4)])
        vc(D("r3"), IND(D("r2"), L1))
        vt(D("rl"), IND(D("r3"), L1), D("mdg"), A.mult); sa(D("r4"), IND(D("r3"), L1), F.Copy)
        sa(D("l64"), D("pu", 0, 1), F.Copy, 0.0, 0.015625); sa(D("l8k"), D("pu", 0, 1), F.Copy, 0.0, 8192.0); sa(D("lcol"), D("pu", 0, 1), F.Copy)
        sa(D("zc"), IND(D("cut"), D("zl")), F.Copy)
        vscan(D("sl"), D("rst"), D("rl"), 0.0, A.mult, A.add)
        vc(L4, D("sl", 15, 64, 16))
        vs(D("sp"), D("kp"), D("l64"), A.mult, -0.4921875, A.add)
        vc(D("r8"), IND(D("r4"), L4))
        places(0)
        vc(D("r12"), IND(D("r8"), L4))
        places(1)
        vt(D("rl2"), IND(D("r12"), L4), D("mdg"), A.mult); sa(D("r16"), IND(D("r12"), L4), F.Copy)
        for q in range(4): sa(D("lb%d" % q), D("blk"), F.Identity, 0.0, D("lenl", q, q + 1))
        places(2)
        vscan(D("sl2"), D("rst"), D("rl2"), 0.0, A.mult, A.add)
        places(3)
        vc(L16, D("sl2", 15, 64, 16))
        places(4)
        sa(D("wa", 0, np_), D("pp", 0, np_), F.Relu, D("l8k"), -8192.0)
        sa(D("pv", 0, np_), D("wa", 0, np_), F.Relu, D("lcol"), -1.0)
        vc(D("r32"), IND(D("r16"), L16))
        vx(D("cr"), D("zc"))
        vc(D("r48"), IND(D("r32"), L16))
        vt(D("pu", 64, 128), D("cr"), D("ej"), A.add); sa(D("pu", 128, 192), D("pu", 64, 128), F.Copy, 16.0)
        vt(D("rl3"), IND(D("r48"), L16), D("mdg"), A.mult)
        vt(D("kr"), IND(D("r48"), L16), D("jj"), A.add)
        vscan(D("sl3"), D("rst"), D("rl3"), 0.0, A.mult, A.add)
        for q in range(4): vs(D("cc%d" % q), D("kr"), D("sl3", 16 * q + 15, 16 * q + 16), A.subtract, D("qj", q, q + 1), A.is_gt)
        pe(D("ppos", 0, 64), [(D("n75"), D("ones", 0, 64))], [(D("lb%d" % q), D("cc%d" % q)) for q in range(4)])
        vt(D("pq", 0, np_), D("pp", 0, np_), D("pv", 0, np_), A.subtract)
        vt(D("pm"), D("ppos", 0, 64), D("md16"), A.mult)
        vs(D("pi"), D("ppos", 0, 64), 7.5, A.add)
        vscan(D("ps"), D("rst"), D("pm"), 0.0, A.mult, A.add)
        vs(D("pr"), D("pi"), 15, A.bitwise_and)
        for e in range(2): vs(D("tl", 4 * e, 4 * e + 4), D("ps", 15, 64, 16), float(ROUND), A.add, float(e - ROUND), A.add)
        vs(D("mlt", 0, 64), D("pr"), D("rcol"), A.is_le)
        for e in range(2): vt(D("vv", 64 * e, 64 * e + 64), D("pu", 64 * e + 64, 64 * e + 128), D("pr"), A.subtract)
        vt(IND(D("dw"), D("tl")), D("vv"), D("mlt"), A.mult)
        if not last: vt(D("lm"), D("pq", nk_, np_), D("mdg"), A.mult)
        for lo, hi in ((0, LAY0), (LAY0, 256)): sa(D("dk", lo, hi), D("dw", lo, hi), F.Copy, 16.0, -65536.0)
        vc(D("kl", 0, nk_), D("pq", 0, nk_))
        vscan(D("ls", 0, LAY0), D("dk", 0, LAY0), D("dw", 0, LAY0), 0.0, A.add, A.max)
        if not last: vscan(D("lsc"), D("rst"), D("lm"), 0.0, A.mult, A.add)
        vs(D("lay", 0, LAY0), D("ls", 0, LAY0), -32.0, A.add, 4095.0, A.min)
        vscan(D("ls", LAY0, 256), D("dk", LAY0, 256), D("dw", LAY0, 256), D("ls", LAY0 - 1, LAY0), A.add, A.max)
        if not last: vc(D("lx"), D("lsc", 15, 64, 16))
        vs(D("lay", LAY0, 256), D("ls", LAY0, 256), -32.0, A.add, 4095.0, A.min)
        sa(D("xp", 0, 16 * LAY0), IND(D(X), D("lay", 0, LAY0)), F.Copy)
        sa(D("xp", 16 * LAY0, 16 * LAYS[t]), IND(D(X), D("lay", LAY0, LAYS[t])), F.Copy)
        vc(D("xp", 16 * LAYS[t], 4096), IND(D(X), D("lay", LAYS[t], 256)))
        w = WIDTH[t]

        def ahead():
            XK = "xk%d" % t; XLN = "xl%d" % (t + 1)
            vc(D(XK), IND(D("xp"), D("lx")))
            sync_for("g", [], D(XK, 0, 48)[1])
            trs = []
            for k in range(3):
                d = T.cores[(rank + k + 1) % n_ranks]
                rid, pid = topo.addr(d, core)
                en = topo.engines(core, d)
                trs.append(RemoteDMATransfer(dst_ids=[DstId(rid=rid, pnc=pid)], dma_engine_mask=(1 << en[2 * k]) + (1 << en[2 * k + 1]), remote_sem=T.sem["xs%d" % (t + 1)],
                                             src=T[XK][:, 16 * k:16 * k + 16], dst=T[XLN][:, 16 * rank:16 * rank + 16]))
            g.remote_dma_fused(trs, local_sem=T.sem.tx)
            sent[0] += 6
            source("XS%d" % (t + 1), "xs%d" % (t + 1), 6, [(XLN, 16 * p, 16 * p + 16, 1) for p in range(n_ranks) if p != rank])
            vc(D(XLN, 16 * rank, 16 * rank + 16), D(XK, 48, 64))

        def kids(buf, o, a, n):
            vc(D(buf, o, o + n // 2), IND(D("xp"), D("kl", a // 16, a // 16 + n // 32)))
            sa(D(buf, o + n // 2, o + n), IND(D("xp"), D("kl", a // 16 + n // 32, a // 16 + n // 16)), F.Copy)
        for i, k, lo, on, by, h in pieces(t):
            kids(SRC[t], k * w + lo, k * w + lo, on + by); send(t, i, k, lo, on, by, h)
            if i == 0 and not last: ahead()
        if last: kids(DST[t], rank * w, 3 * w, w)

    for k in range(4):
        p = rank if k == 0 else arrival(2, k - 1)
        sync_for("ys"[k % 2], [], D("yb", p * 512, p * 512 + 512)[1])
        queue["ys"[k % 2]].dma_start(T.y[:, p * 512:p * 512 + 512], T.yb[:, p * 512:p * 512 + 512]).then_inc(T.sem.stor, 16)
    g.sync.wait_ge(T.sem.stor, 64)
    g.wait_ge(T.sem.tx, sent[0])
    for q in ("v", "s", "t", "g"):
        wait("g", q, count[q])
